import numpy as np, ml_dtypes
CORES = [3,7,11,15,131,135,139,143]
N = 8
BF = ml_dtypes.bfloat16
def gentries(a):
    return np.ascontiguousarray(a.reshape(8, 16, -1).transpose(0, 2, 1)).reshape(8, -1)
def gtable(e):
    e = np.asarray(e); return np.ascontiguousarray(e.reshape(8, -1, 16).transpose(0, 2, 1)).reshape(128, -1).astype(np.int32)
W, P, M, L, TV = 2048, 256, 16, 1, 3
def parts(rng):
    X = rng.integers(0, 256, (N, 8, 16, W))
    cen = rng.integers(0, 256, (N, 8, 16, 32)); pick = rng.integers(0, 32, (N, 8, 1, W))
    near = np.clip(np.take_along_axis(cen, pick, 3) + rng.integers(-20, 21, (N, 8, 16, W)), 0, 255)
    X[:, 1::2] = near[:, 1::2]
    Q = rng.integers(0, W, (N, 8, 16, W)); R = rng.integers(0, W, (N, 8, 16, P))
    R = np.where(rng.random((N, 8, 1, P)) < 0.0625, R[:, :, :1], R)
    return X, Q, R, rng.integers(1, 256, (N, 8, 16, 1)), rng.integers(0, 2048, (N, 8, M))
def pack(X, Q, R, w, ka):
    return {"xf": np.ascontiguousarray(X.reshape(N, 128, W)).astype(np.float32).astype(BF), "pa": np.ascontiguousarray(Q.reshape(N, 128, W)).astype(np.int32),
            "rp": np.ascontiguousarray(R.reshape(N, 128, P)).astype(np.int32), "wt": np.ascontiguousarray(w.reshape(N, 128, 1)).astype(np.int32), "kap": np.stack([gtable(a) for a in ka])}
def setup_inputs(rng):
    return pack(*parts(rng))
def setup_inputs_corners(rng):
    X, Q, R, w, ka = parts(rng); n = np.arange(W)[None, :]; k = np.arange(16)[:, None]; turn = int(rng.integers(0, 8))
    for a in range(N):
        for g in range(8):
            kind = (a + g + turn) % 8
            if kind == 0: Q[a, g] = n; w[a, g] = 255
            if kind == 1: Q[a, g] = 0; R[a, g, ::2] = 0
            if kind == 2: Q[a, g] = W - 1; R[a, g, 1::2] = W - 1
            if kind == 3: X[a, g] = int(rng.choice(np.array([0, 255, 100])))
            if kind == 4: ka[a, g] = ka[a, g, :1]
            if kind == 5: w[a, g] = 1; ka[a, g] = 0; ka[a, g, M - 1] = 2047
            if kind == 6: R[a, g] = R[a, g, :, :1]
            if kind == 7:
                R[a, g] = (R[a, g, :1] + k) & (W - 1); Q[a, g] = (n + k - 15) & (W - 1); X[a, g, :, 1::2] = X[a, g, :, ::2]
    q = int(rng.integers(0, N)); R[q] = R[q][:, :1].copy()
    return pack(X, Q, R, w, ka)
def setup_inputs_crowd(rng):
    X, Q, R, w, ka = parts(rng); o = rng.permutation(N); H = W // 4; B = W // P; hit = np.zeros((N, 8, P), bool)
    for a in range(N):
        for g in range(8):
            kind = int(rng.integers(0, 4)); hit[a, g] = (True, True, False, False)[kind]
            if kind == 1: hit[a, g, rng.integers(0, P)] = False
            if kind == 2: hit[a, g] = rng.random(P) < 0.5
    hit[o[0]] = True; hit[o[1]] = True; hit[o[1], rng.integers(0, 8), rng.integers(0, P)] = False
    hit[o[2]] = False; hit[o[3]] = False; hit[o[3], rng.integers(0, 8), rng.integers(0, P)] = True
    many = np.add.reduce(hit.reshape(N, 8 * P).astype(np.int64), axis=1); t = (int(o[2]) + 1) % N
    for g in range(8):
        for d in range(N):
            a = (t + d) % N; v = rng.integers(60, 190, 16); s = v + rng.choice(np.array([-50, 50]), 16); col = rng.permutation(W); plain = col[:H]
            if d == N - 1:
                plain, loc = keep
                X[a, g][:, plain] = v[:, None]; X[a, g][:, loc] = v
                R[a, g] = plain[rng.integers(0, H, (16, P))]; R[a, g, 1] = loc
                continue
            us = int(np.add.reduce(w[a, g, :, 0] * s)) & (W - 1); uv = int(np.add.reduce(w[a, g, :, 0] * v)) & (W - 1)
            z = ((us * us) >> 5) + int(ka[a, g, 0]) * us; c = z & (W - 1); c1 = (z + int(many[a])) & (W - 1)
            rest = col[H:]; rest = rest[(rest % B != us % B) & (rest % B != uv % B) & (rest != c) & (rest != c1)]; loc = int(rest[0])
            if d == 0: keep = (plain, loc)
            X[a, g][:, plain] = v[:, None]; X[a, g][:, c] = v; X[a, g][:, c1] = v; X[a, g][:, loc] = s; Q[a, g, 0, c] = plain[0]; Q[a, g, 0, c1] = plain[0]
            R[a, g] = plain[rng.integers(0, H, (16, P))]; R[a, g, 1] = np.where(hit[a, g], loc, R[a, g, 1])
    return pack(X, Q, R, w, ka)
def setup_inputs_ends(rng):
    X = 255 * rng.integers(0, 2, (N, 8, 16, W)); rec = 255 * rng.integers(0, 2, (N, 8, 1, W)); Q = (W - 1) * rng.integers(0, 2, (N, 8, 16, W))
    w = 1 + 254 * rng.integers(0, 2, (N, 8, 16, 1)); ka = 2047 * rng.integers(0, 2, (N, 8, M)); ka[:, :, 0] = 0; ka[:, :, M - 1] = 2047
    lo = (W - 1) * rng.integers(0, 2, (N, 8, 1, P))
    for a in range(N):
        for g in range(8): lo[a, g, 0, P - 1] = 0 if (a + g + 2) % 4 in (0, 1) else W - 1
    hi = W - 1 - lo; k = np.arange(16)[:, None]
    kind = rng.integers(0, 4, (N, 8, 1, P)); kind[..., P - 1] = 2; q = rng.integers(0, 16, (N, 8, 1, P))
    R = (W - 1) * rng.integers(0, 2, (N, 8, 16, P))
    R = np.where(kind == 1, np.where(k <= q, lo, hi), R); R = np.where(kind == 2, np.where(k == 1, hi, lo), R); R = np.where(kind == 3, rng.integers(0, W, (N, 8, 16, P)), R)
    for a in range(N):
        for g in range(8):
            role = (a + g + 2) % 4
            if role == 0 or role == 2:
                X[a, g] = rec[a, g]; X[a, g, :, 0] = 0 if role == 0 else 255; X[a, g, :, W - 1] = 255 - X[a, g, :, 0]
                if role == 0: w[a, g] = 255
                else:
                    u = (255 * int(np.add.reduce(w[a, g, :, 0]))) & (W - 1)
                    for kk in (0, 2047):
                        c = (((u * u) >> 5) + kk * u) & (W - 1)
                        if 0 < c < W - 1: X[a, g, :, c] = 255; Q[a, g, :, c] = W - 1
            else:
                o = rng.permutation(16); w[a, g, o[0], 0] = 255; w[a, g, o[1], 0] = 1; w[a, g, o[2], 0] = 1; top = W - 1 if role == 1 else 0
                v = np.zeros(16, np.int64); v[o[:3]] = 255; X[a, g, :, top] = v; X[a, g, :, W - 1 - top] = 255 - v
                if role == 1: ka[a, g] = 0; ka[a, g, M - 1] = 2047
                else:
                    f = 2 if g < 4 else 3; u = W - 1
                    ka[a, g, :f] = 0; ka[a, g, f] = 2047; ka[a, g, f + 1] = 1
                    for kk, i in ((0, -1), (2047, int(o[3])), (1, int(o[4]))):
                        c = (((u * u) >> 5) + kk * u) & (W - 1)
                        X[a, g, :, c] = v; Q[a, g, 0, c] = W - 1
                        if i >= 0: X[a, g, i, c] = 255 - v[i]
    return pack(X, Q, R, w, ka)
def setup_inputs_spread(rng):
    X, Q, R, w, ka = parts(rng); e = rng.choice(np.array([1, 2, 4, 8]), (N, 8, 1, 1)); back = rng.random((N, 8, 1, 1)) < 0.5
    X = np.minimum((np.exp2(8 * rng.random((N, 8, 1, W))) * np.exp2(-3 * rng.random((N, 8, 16, 1))) * (0.5 + rng.random((N, 8, 16, W)))).astype(np.int64), 255)
    Q = np.minimum((W * rng.random((N, 8, 16, W)) ** e).astype(np.int64), W - 1); Q = np.where(back, W - 1 - Q, Q)
    R = np.minimum((W * rng.random((N, 8, 16, P)) ** e[:, ::-1]).astype(np.int64), W - 1); R = np.where(back, R, W - 1 - R)
    w = np.minimum(np.exp2(8 * rng.random((N, 8, 16, 1))).astype(np.int64), 255); ka = np.minimum(np.exp2(11 * rng.random((N, 8, M))).astype(np.int64) - 1, 2047)
    return pack(X, Q, R, w, ka)
def brink(rng, X, Q, R, w, ka):
    pl = 4093 & (W - 1); v = rng.integers(60, 190, 16); w[0] = 16; w[1] = 1; ka[0] = 1929; ka[1] = 815
    goal = [4081 & (W - 1), 5]
    cs = [(((goal[m] * goal[m]) >> 5) + int(ka[m]) * goal[m]) & (W - 1) for m in range(2)]
    col = rng.permutation(W); col = col[(col != pl) & (col != cs[0]) & (col != cs[1]) & (col > 0) & (col < W - 1)][:5]
    X[:, pl] = v
    for m in range(2):
        s = v + rng.choice(np.array([-50, 50]), 16); rest = (goal[m] - int(np.add.reduce((w[:, 0] * s)[2:]))) & (W - 1); s[0] = rest >> 4; s[1] = rest & 15
        X[:, col[m]] = s; X[:, cs[m]] = v; Q[0, cs[m]] = pl; R[:, m::4] = pl; R[1, m::4] = col[m]
    X[:, col[2]] = 0; X[:, col[3]] = 255; X[:, col[4]] = 255; X[int(rng.integers(0, 16)), col[4]] = 254
    for j, way in ((2, (4, 2, 2, 3)), (3, (2, 4, 3, 2))):
        for k in range(4): R[k + 1, j::4] = col[way[k]]
def setup_inputs_ties(rng):
    X, Q, R, w, ka = parts(rng); turn = int(rng.integers(0, 8))
    for a in range(N):
        for g in range(8):
            if (a + g + turn) % 8 == 7:
                brink(rng, X[a, g], Q[a, g], R[a, g], w[a, g], ka[a, g])
                continue
            top = int(rng.choice(np.array([1, 2, 3]))); o = rng.permutation(16)[:3]; v = rng.integers(0, 252, 16)
            X[a, g] = v[:, None]; X[a, g, o] = v[o][:, None] + rng.integers(0, top + 1, (3, W))
    return pack(X, Q, R, w, ka)
def check_inputs(d):
    bad = []
    for k, lo, hi in (("xf", 0, 255), ("pa", 0, W - 1), ("rp", 0, W - 1), ("wt", 1, 255), ("kap", 0, 2047)):
        v = np.asarray(d[k]).astype(np.float64)
        if not np.all((v >= lo) & (v <= hi)): bad.append("range of " + k)
        elif not np.all(v == np.floor(v)): bad.append("whole numbers in " + k)
    return bad
def reference(xf, pa, rp, wt, kap):
    X = xf.astype(np.float32).astype(np.int32).reshape(N, 8, 16, W); Q = pa.astype(np.int64).reshape(N, 8, 16, W); R = rp.astype(np.int64).reshape(N, 8, 16, P)
    w = wt.astype(np.int64).reshape(N, 8, 16, 1); ka = np.stack([gentries(a) for a in kap]).astype(np.int64); A = np.zeros(N, np.int64)
    k = np.arange(16)[:, None]; B = W // P
    for v in range(TV):
        S = np.roll(R, v, axis=0)
        x = np.take_along_axis(X, S.reshape(N, 8, 1, 16 * P), 3).reshape(N, 8, 16, 16, P)
        D = np.add.reduce(np.abs(x[:, :, :, 2:16 - L] - x[:, :, :, 1:15 - L]), axis=2)
        p = 1 + np.argmax(D, axis=2)
        xt = [np.take_along_axis(x, (p + j)[:, :, None, None, :], 3)[:, :, :, 0] for j in range(L + 1)]
        u = np.add.reduce(w * xt[0], axis=2) & (W - 1)
        c = (((u * u) >> 5)[:, :, None] + ka[..., None] * u[:, :, None] + A[:, None, None, None]) & (W - 1)
        anc = np.take_along_axis(Q, c.reshape(N, 8, 1, M * P), 3).reshape(N, 8, 16, M, P)
        b = np.take_along_axis(anc, (p - 1)[:, :, None, None, :], 2)[:, :, 0]
        pk = p[:, :, None]
        cc = np.concatenate([np.take_along_axis(S, pk, 2), c], axis=2); bb = np.concatenate([np.take_along_axis(S, pk - 1, 2), b], axis=2)
        Xc = np.take_along_axis(X, cc.reshape(N, 8, 1, -1), 3).reshape(N, 8, 16, M + 1, P); Xb = np.take_along_axis(X, bb.reshape(N, 8, 1, -1), 3).reshape(N, 8, 16, M + 1, P)
        E = np.zeros((N, 8, M + 1, P), np.int64)
        for j in range(1, L + 1):
            E = E + np.add.reduce(np.abs(Xc + j * (Xc - Xb) - xt[j][:, :, :, None, :]), axis=2)
        m = np.argmin(E, axis=2)
        win = np.take_along_axis(cc, m[:, :, None], 2)
        pre = np.take_along_axis(anc, np.maximum(m - 1, 0)[:, :, None, None, :], 3)[:, :, :, 0]
        late = (((S * win) >> 5) + S + 37 * k) & (W - 1)
        new = np.where(k < pk, pre, np.where(k == pk, win, np.where(k > pk + L, late, S)))
        S2 = np.where((m > 0)[:, :, None], new, S)
        mid = (np.take_along_axis(Xc, m[:, :, None, None, :], 3)[:, :, :, 0] + xt[1]) >> 1
        n = np.broadcast_to((B * np.arange(P) + (u & (B - 1)))[:, :, None], (N, 8, 16, P))
        np.put_along_axis(Q, n, S2, 3); np.put_along_axis(X, n, mid, 3)
        A = np.add.reduce((m > 0).astype(np.int64).reshape(N, 8 * P), axis=1)
        R = np.roll(S2, -v, axis=0)
    return {"yr": R.reshape(N, 128, P).astype(np.float32), "yq": np.add.reduce((k + 1) * Q, axis=2).astype(np.float32), "yx": np.add.reduce((k + 1) * X, axis=2).astype(np.float32)}

@@ -1,0 +1,578 @@
+import numpy as np
+from concourse.mybir import AluOpType, ActivationFunctionType
+
+ALU = AluOpType
+ACT = ActivationFunctionType
+W, P, TV, H = 2048, 256, 3, 128
+XF = 3 * H
+MD = 2
+F32, BF, F16, I32, U16 = "float32", "bfloat16", "float16", "int32", "uint16"
+
+SCRATCH = {
+    "X0": ("sbuf", [128, XF + W], BF), "X1": ("sbuf", [128, XF + W], BF), "Q0": ("sbuf", [128, H + W], I32), "Q1": ("sbuf", [128, H + W], I32),
+    "NUM": ("sbuf", [128, H + W], F32), "Y": ("sbuf", [128, W], F32), "Q16": ("sbuf", [128, W], F16),
+    "Qk": ("sbuf", [128, W], I32), "Xk": ("sbuf", [128, W], BF),
+    "x": ("sbuf", [128, 4096], BF), "ab": ("sbuf", [128, 2 * 13 * H], BF), "am": ("sbuf", [128, 4096], F16),
+    "Xc": ("sbuf", [128, 4096], BF), "Xb": ("sbuf", [128, 4096], BF), "mx": ("sbuf", [128, 2 * 17 * H], F16),
+    "rp32": ("sbuf", [128, P], I32), "R0": ("sbuf", [128, P], U16), "R1": ("sbuf", [128, P], U16), "R2": ("sbuf", [128, P], U16),
+    "O0": ("sbuf", [128, P], U16), "O1": ("sbuf", [128, P], U16), "Of": ("sbuf", [128, P], F32), "Rf": ("sbuf", [128, P], F32),
+    "R16": ("sbuf", [128, P], F16), "s1": ("sbuf", [128, 208], I32), "ri": ("sbuf", [128, 16], I32),
+    "eqT": ("sbuf", [128, P], BF), "rT": ("sbuf", [128, P], BF), "mask": ("sbuf", [128, 2 * MD * H], BF), "pl": ("sbuf", [128, 48], U16),
+    "ur": ("sbuf", [128, 16], I32), "u": ("sbuf", [128, 16], I32), "uu": ("sbuf", [128, 16], F32), "ua": ("sbuf", [128, 16], I32),
+    "z1": ("sbuf", [128, 288], F32), "z2": ("sbuf", [128, 288], I32), "CL": ("sbuf", [128, 288], I32), "cl": ("sbuf", [128, P], U16),
+    "bl": ("sbuf", [128, P], U16), "H0": ("sbuf", [128, P], F32), "Hh": ("sbuf", [128, P], F32),
+    "s2": ("sbuf", [128, 288], I32), "twi": ("sbuf", [128, 16], I32), "tT": ("sbuf", [128, P], BF),
+    "sb": ("sbuf", [128, 288], F32), "cwf": ("sbuf", [128, 288], F32), "cw": ("sbuf", [128, 16], U16),
+    "t1": ("sbuf", [128, P], F32), "t2": ("sbuf", [128, P], I32), "t3": ("sbuf", [128, P], F32), "t4": ("sbuf", [128, P], I32),
+    "S2": ("sbuf", [128, P], I32), "m1": ("sbuf", [128, P], F16), "m2": ("sbuf", [128, P], I32), "m16": ("sbuf", [128, P], F16),
+    "ys": ("sbuf", [128, P], F32), "u7": ("sbuf", [128, 16], I32), "n32": ("sbuf", [128, 16], I32), "nl": ("sbuf", [128, 16], U16),
+    "sg": ("sbuf", [128, 16], BF), "aj": ("sbuf", [128, 16], F32), "Acol": ("sbuf", [128, 4], F32),
+    "wk": ("sbuf", [128, 16], I32), "col": ("sbuf", [128, 24], F32), "pI": ("sbuf", [128, 8], I32),
+    "D0": ("sbuf", [128, 128], F32), "KK": ("sbuf", [128, 128], BF), "G16": ("sbuf", [128, 128], BF), "C144": ("sbuf", [128, 144], BF),
+    "q18": ("sbuf", [128, 144], BF), "t18": ("sbuf", [128, 144], BF), "sm": ("sbuf", [128, 128], F32), "smi": ("sbuf", [128, 16], I32),
+    "II": ("sbuf", [128, MD * 128], BF), "nI": ("sbuf", [128, 128], BF), "I2": ("sbuf", [128, 128], BF), "BLK": ("sbuf", [128, 128], BF),
+    "ones": ("sbuf", [128, 128], BF), "b8": ("sbuf", [128, 48], BF),
+    "Sel": ("sbuf", [128, 144], BF), "Wsel": ("sbuf", [128, 288], BF), "LBb": ("sbuf", [128, 144], BF),
+    "LBf": ("sbuf", [128, 144], F32), "db": ("sbuf", [128, 128], BF), "eqtab": ("sbuf", [128, 128], BF),
+    "L1": ("sbuf", [128, 48], F16), "Z1": ("sbuf", [128, 288], BF), "Z2": ("sbuf", [128, 288], BF), "kd": ("sbuf", [128, 288], F16),
+    "KapT": ("sbuf", [128, 288], F32), "NC": ("sbuf", [128, 16], F32), "lists": ("sbuf", [128, 32], U16),
+    "c1": ("sbuf", [128, 104], F32), "c2": ("sbuf", [128, 144], F32), "tm": ("sbuf", [128, 32], F32), "tb": ("sbuf", [128, 640], BF),
+    "F": ("sbuf", [128, 768], BF),
+}
+for _b in range(8):
+    SCRATCH["p%d" % _b] = ("psum", [128, 512], F32)
+DMAS = [a + str(h) for a in ("lx", "lr", "lq", "lw", "lk", "oq", "ox", "or", "kq", "kx", "ex0", "ex1", "eq0", "eq1") for h in range(2)]
+SEMAPHORES = ["cV", "cS", "cP", "cG", "sent"] + DMAS + ["ar%d%d" % (v, h) for v in range(TV) for h in range(2)]
+
+COST = {"CY": 1.04, "GA": 1.55, "SC": 3.5, "PE": 0.52, "TT2": 1.0, "HOP": 120.0, "SAME": 70.0, "LINK": 2600.0, "TG": 0.0}
+WIDTH = {F32: 4, I32: 4, BF: 2, F16: 2, U16: 2}
+PAR = {"d": ["SSSS"] * 6, "e": ['SVVVS', 'SVVSV', 'SSVSV', 'SVSVV', 'SVVVS', 'SVVVS'], "lead": 5000.0, "look": 100.0, "bias": {}, "rounds": 1, "vpen": 300.0}
+KEY = "0g060v0t1o1r1p17191f0201080a131512362u10295v50143c1c0s11240x0z0y161a1l5d5wjt1j30331ik70i221kk6282i3d5y2d3v2q1n2p2o2n2r39egjf253a3e183m0r2f1z1v311u1m1w261y5jiv03090k070b0j0d0e0p0f0m20211t1h544z4n7k000o0h0c04050l0q1d0n0u2a1s1x2b1b1g1q231e2e2t2h2v2z2w3h323l2l2j270w2g3g3j3q493w463x5x486k6r6w3y3o444r3p3t2x38474e4m4j4d4f4h4l4s4x5a534342574g4o5851555h5c5g5m5f5k5o5q5r5t6266696b6d6g6l6q6t6v6z706h6m8q6y728e8r2m2k2c2s2y3b3s353f3u3i3k3z3r3n343740414a4b4q4c454i4k4p4t4v4u4w4y5259567h5u645z7t617y828m5s5n60675b5l5e5i656a6e6p63686c5p6o6s6u776f6j736i6n716x757b74797c787a7d7f7g7j7m7o7p767s7u7w7x8184878d7r8397808c86al8x927i7n7l7q7v7e8g7z898j8b85888a8h8i8l8n8p8w8o8y8s8u969093958f94989a9b9d9ca98z9h8kbg9mc1bvbma69iah9v9j9g9l9t9za39sab9q9r9xa2adanaqb29f9naxapazbaaearbeb7bdbib4akb5blbpbrc0c5c8cfcdcgciclckcacbchc2cnedcscvdycucxde8t918v999e9pa19k9oa49wa0a59u9ya7a8aaacafajb3agaib9asauavayawb6aob8amb1d2atbkbhd8bqdwdsdvbsbococcbbbfbjbnbtbwbxc4bubyc3c6cjcmcqd4bcb0crbzc7cwc9cecyctczd0cpd1d3d5d6d7dddfdhdjdidkdodrdue8eaeidze9ebe7ehfve1dmeke6efdad9e3dpdxe4eje5dle0dndtdgdqdce2eldbeeeoeqepeteuereyf2f5f7f8fcfbfjfmevipf0f3f6ilf9jljnjremesenecexfaftfxg0gafpfsfufng1g6gggjfwfzg4gcgmgph2grfffkhfgfgnhggigshmgvguhdh3h9hpi1i2i8iaj7iyj0j2jdjgiwjojqjyjuk0k4k2k5k3jvjzjwewf1ezf4feflg3fdfgfyfhfrg2fofqg5g7g9gbgdgkgoglg8gtgwh0gxgzh1h4hcgyh8h6iqhehshij4hvjpjsk1figegqghhbhthjhuhni0hkhhh7hlhyi3i5hqhohrhwhzi6ibijidh5haiehxiciii4ihirifiojeiniti7i9ixigikimiuj6j8jaisizj1j3j5jbjijjjkjmjhjcjxj9"
+PAR["key"] = [int(KEY[_i:_i + 2], 36) for _i in range(0, len(KEY), 2)]
+
+
+def build(T, send):
+    ops = []
+    CY, GA, SC, PE = COST["CY"], COST["GA"], COST["SC"], COST["PE"]
+    tag = [0, 0]
+
+    def v(name, lo=0, hi=None, st=1):
+        return (name, lo, SCRATCH[name][1][1] if hi is None else hi, st)
+
+    def ap(a):
+        if isinstance(a, tuple) and a[0] == "ind":
+            return ap(a[1]).indirect(ap(a[2]))
+        if isinstance(a, tuple):
+            return T[a[0]][:, a[1]:a[2]:a[3]] if a[3] != 1 else T[a[0]][:, a[1]:a[2]]
+        return a
+
+    def ind(win, off):
+        return ("ind", win, off)
+
+    def views(xs):
+        out = []
+        for a in xs:
+            if isinstance(a, tuple):
+                out += [a[1], a[2]] if a[0] == "ind" else [a]
+        return out
+
+    def n_of(a):
+        if a[0] == "ind":
+            return 16 * (a[2][2] - a[2][1])
+        return (a[2] - a[1] + a[3] - 1) // a[3]
+
+    def add(eng, fns, outs, ins, cost, **kw):
+        w, r = [], views(ins)
+        for o in outs:
+            if o[0] == "ind":
+                w.append(o[1]); r.append(o[2])
+            else:
+                w.append(o)
+        d = {"eng": eng, "fns": fns, "w": w, "r": r, "cost": cost, "half": tag[1]}
+        d.update(kw)
+        ops.append(d)
+        return d
+
+    def vcost(out, ins, tt=False):
+        n = n_of(out)
+        if out[0] == "ind":
+            return 50 + n * SC * CY
+        if ins[0][0] == "ind":
+            return 50 + n * max(GA, COST["TG"] if tt else 0.0) * CY
+        two = all(WIDTH[SCRATCH[a[0]][2]] == 2 for a in views([out] + ins))
+        c = 1.0
+        if tt and not any(SCRATCH[a[0]][0] == "psum" for a in views(ins)):
+            c = COST["TT2"] if two else 2.0
+        elif two:
+            c = 0.5
+        return max(64, n * c) * CY
+
+    def cp(out, in_):
+        return add("V", [lambda q: q.tensor_copy(ap(out), ap(in_))], [out], [in_], vcost(out, [in_]))
+
+    def tt(out, a, b, op):
+        return add("V", [lambda q: q.tensor_tensor(ap(out), ap(a), ap(b), op)], [out], [a, b], vcost(out, [a, b], True))
+
+    def ts(out, a, s1, op0, s2=None, op1=None):
+        if op1 is None:
+            f = lambda q: q.tensor_scalar(ap(out), ap(a), ap(s1), None, op0)
+        else:
+            f = lambda q: q.tensor_scalar(ap(out), ap(a), ap(s1), ap(s2), op0, op1)
+        return add("V", [f], [out], [a, s1, s2], vcost(out, [a]))
+
+    def scan(out, d0, d1, op0, op1):
+        return add("V", [lambda q: q.tensor_tensor_scan(ap(out), ap(d0), ap(d1), 0.0, op0, op1)], [out], [d0, d1], max(64, n_of(out)) * CY)
+
+    def ms(out, c):
+        return add("V", [lambda q: q.memset(ap(out), c)], [out], [], max(64, n_of(out) * WIDTH[SCRATCH[out[0]][2]] / 4) * CY)
+
+    def act(out, in_, func, bias=None, scale=None, acc=None):
+        kw = {}
+        if bias is not None: kw["bias"] = bias
+        if scale is not None: kw["scale"] = scale
+        if acc is not None: kw["accum_out"] = acc
+        f = lambda q: q.activation(ap(out), ap(in_), func, **{k: ap(a) for k, a in kw.items()})
+        n = n_of(out)
+        return add("S", [f], [out] + ([acc] if acc else []), [in_, bias, scale], 65 + n * GA * CY if in_[0] == "ind" else max(64, n) * CY)
+
+    def gather(out, in_, scale=None):
+        a = cp(out, in_) if scale is None else ts(out, in_, scale, ALU.mult)
+        ops.pop()
+        b = act(out, in_, ACT.Copy, scale=scale)
+        b["opt"] = {"S": (b["fns"], b["cost"]), "V": (a["fns"], a["cost"])}
+        return b
+
+    def mm(groups):
+        fns, outs, ins, cost = [], [], [], 0.0
+        for out, terms in groups:
+            outs.append(out)
+            for i, (l, r) in enumerate(terms):
+                fns.append(lambda q, o=out, l=l, r=r, a=(i == 0), z=(i == len(terms) - 1): q.matmul(ap(o), ap(l), ap(r), a, z))
+                ins += [l, r]
+                cost += max(64, n_of(r)) * PE * (4 if SCRATCH[l[0]][2] == F32 else 1)
+        return add("P", fns, outs, ins, cost)
+
+    def iota(out, pattern, base, cm):
+        if SCRATCH[out[0]][2] == I32:
+            f = lambda q: q.iota(ap(out), pattern, base, cm)
+        else:
+            f = lambda q: q.iota(ap(out), pattern, base, cm, allow_small_or_imprecise_dtypes=True)
+        return add("G", [f], [out], [], 130 + 2 * n_of(out) * CY)
+
+    def keep(out, in_, op, base, sign):
+        return add("G", [lambda q: q.affine_select(ap(out), ap(in_), [[sign, 128]], op, 0.0, base, -sign)], [out], [in_], 170 + 256 * CY)
+
+    def dma(eng, sem, f, outs, ins, lat):
+        return add(eng, [lambda q, a=a: q.dma_start(*f(a)) for a in range(2)], outs, ins, 120.0, sem=sem, lat=lat)
+
+    eq, mul, sub, addo, mn, mxo, band = ALU.is_equal, ALU.mult, ALU.subtract, ALU.add, ALU.min, ALU.max, ALU.bitwise_and
+    Xs, Qs = [v("X%d" % h, XF) for h in range(2)], [v("Q%d" % h, H) for h in range(2)]
+    K = W // 2
+
+    def rows(a):
+        return slice(64 * a, 64 * a + 64)
+
+    for h in range(2):
+        dma("S", "lr%d" % h, lambda a, h=h: (T.rp32[rows(a), H * h:H * h + H], T.rp[rows(h), H * a:H * a + H]), [v("rp32", H * h, H * h + H)], [], 2200)
+        dma("Y", "lx%d" % h, lambda a, h=h: (T["X%d" % h][rows(a), XF:], T.xf[rows(h), :]), [Xs[h]], [], 3200 + 1800 * h)
+    for h in range(2):
+        dma("Y", "lw%d" % h, lambda a, h=h: (T.wk[rows(a), 4 * h:4 * h + 1], T.wt[rows(h), :]), [v("wk", 4 * h, 4 * h + 4)], [], 5000)
+        dma("Y", "lk%d" % h, lambda a, h=h: (T.wk[rows(a), 8 + 4 * h:9 + 4 * h], T.kap[rows(h), :]), [v("wk", 8 + 4 * h, 12 + 4 * h)], [], 5000)
+    for h in range(2):
+        dma("Y", "lq%d" % h, lambda a, h=h: (T["Q%d" % h][rows(a), H:], T.pa[rows(h), :]), [Qs[h]], [], 9000 + 4000 * h)
+
+    iota(v("D0"), [[1, 128]], 0, -1)
+    iota(v("pI", 0, 1), [[0, 1]], 0, 1)
+    iota(v("sm", 0, 24), [[0, 3], [1, 8]], 0, 0)
+    iota(v("KK"), [[0, 8], [1, 16]], 0, 0)
+    iota(v("sm", 32, 48), [[2, 2], [0, 8]], 12, 16)
+    iota(v("sm", 48, 56), [[0, 8]], 13, 16)
+    iota(v("C144"), [[1, 144]], -15, 0)
+    iota(v("q18"), [[1, 8], [0, 18]], 0, 0)
+    iota(v("t18"), [[0, 8], [1, 18]], 0, 0)
+    iota(v("G16"), [[16, 8], [0, 16]], 0, 0)
+    iota(v("sm", 64, 80), [[1, 16]], 0, 0)
+    iota(v("col", 16, 17), [[0, 1]], -H, 1)
+    iota(v("NUM"), [[1, W + H]], -H, 0)
+    for j in range(MD):
+        ts(v("II", 128 * j, 128 * j + 128), v("D0"), 0.0, eq)
+    Ib, nI = v("II", 0, 128), v("nI")
+    act(nI, Ib, ACT.Copy, scale=-1.0); act(v("I2"), Ib, ACT.Copy, scale=2.0)
+    ts(v("pI", 1, 2), v("pI", 0, 1), 15, band)
+    ts(v("pI", 2, 3), v("pI", 0, 1), 4, ALU.arith_shift_right)
+    ts(v("pI", 3, 4), v("pI", 0, 1), 7, band)
+    ts(v("pI", 4, 5), v("pI", 1, 2), 3, ALU.arith_shift_right)
+    ts(v("pI", 5, 6), v("pI", 0, 1), 6, ALU.arith_shift_right)
+    cp(v("col", 0, 6), v("pI", 0, 6))
+    pr, pq, p7, p3, p64 = (v("col", j, j + 1) for j in (1, 2, 3, 4, 5))
+    p16, pr1, yb, pc, pr8, pr8k = (v("col", j, j + 1) for j in (6, 7, 8, 9, 10, 11))
+    act(p16, pq, ACT.Copy, scale=16.0); act(pr1, pr, ACT.Identity, bias=1.0); act(pr8, pr, ACT.Copy, scale=8.0)
+    act(pr8k, p64, ACT.Identity, scale=float(K), bias=pr8)
+    ts(yb, pr, 1.0, eq, -1024.0 * 136, mul)
+    act(pc, p7, ACT.Identity, scale=18.0, bias=p3)
+    cp(v("col", 12, 14), v("wk", 0, 8, 4)); cp(v("col", 14, 16), v("wk", 8, 16, 4))
+    wc, kc = [v("col", 12 + h, 13 + h) for h in range(2)], [v("col", 14 + h, 15 + h) for h in range(2)]
+    q8 = v("sm", 0, 8)
+    b16, bm16, b32, bm32, b64, bm64 = (v("b8", 8 * j, 8 * j + 8) for j in range(6))
+    ts(b16, q8, pq, eq, 16.0, mul)
+    for b, c in ((bm16, -1.0), (b32, 2.0), (bm32, -2.0), (b64, 4.0), (bm64, -4.0)):
+        act(b, b16, ACT.Copy, scale=c)
+    ms(v("c1"), 1.0); ms(v("c1", 0, 104, 13), -1.0e6); ms(v("c2"), -1.0); ms(v("c2", 0, 144, 18), 2.0e7)
+    ms(v("p4", 305, 432, 18), 1.0e7); ms(v("p5", 305, 432, 18), 1.0e7)
+    bc16, bcq, perm = v("lists", 0, 8), v("lists", 8, 17), v("lists", 18, 26)
+    cp(bc16, q8)
+    act(v("eqtab"), v("KK"), ACT.Identity, scale=-1.0, bias=12.0)
+    ts(v("db"), v("KK"), pr, eq)
+    ts(v("L1", 0, 24), v("sm", 0, 24), pq, eq, -1.0, mul)
+    ts(v("sm", 96, 120), v("sm", 0, 24), pq, eq)
+    tt(v("L1", 24, 48), v("sm", 96, 120), v("sm", 32, 56), mul)
+    ts(v("Sel"), v("C144"), p16, eq)
+    act(v("LBb"), v("Sel"), ACT.Copy, scale=pr1); act(v("LBf"), v("Sel"), ACT.Copy, scale=pr1)
+    act(v("tm", 0, 9), v("sm", 64, 73), ACT.Identity, scale=16.0, bias=pr)
+    ts(v("smi", 0, 9), v("tm", 0, 9), 1.0 / 18, mul, 0.5 / 18 - 0.5, addo); cp(bcq, v("smi", 0, 9))
+    act(v("tm", 16, 24), q8, ACT.Identity, scale=2.0, bias=pc); ts(perm, v("tm", 16, 24), 1.0, addo)
+    BLK = v("BLK")
+    ts(BLK, v("G16"), p16, eq)
+    for h in range(2):
+        part = lambda name: v(name, 144 * h, 144 * h + 144)
+        act(part("Wsel"), v("Sel"), ACT.Copy, scale=wc[h])
+        ts(part("kd"), v("t18"), pr1, eq, kc[h], mul)
+        mm([(v("p%d" % (6 + h), 0, 144), [(BLK, part("kd"))])])
+        act(part("KapT"), v("p%d" % (6 + h), 0, 144), ACT.Copy)
+    ms(v("Acol", 0, 1), -0.484375)
+    act(v("NC", 0, 8), q8, ACT.Identity, scale=128.0, bias=pr8k); act(v("NC", 8, 16), q8, ACT.Identity, scale=128.0, bias=pr8)
+    le2, eq1, le0, gtk, kb = (v("tb", 128 * j, 128 * j + 128) for j in range(5))
+    F1, FE, FA, FB, FC, FD = (v("F", 128 * j, 128 * j + 128) for j in range(6))
+    tt(kb, v("KK"), BLK, mul)
+    keep(le2, BLK, ALU.is_ge, 2, -1); keep(eq1, BLK, eq, -1, 1); keep(le0, BLK, ALU.is_ge, 0, -1); keep(gtk, kb, ALU.is_ge, -3, 1)
+    for o, i, c in ((F1, le2, -4096.0), (FE, eq1, 32.0), (FA, gtk, -32.0), (FB, gtk, -5.0), (FC, le0, 32768.0), (FD, eq1, -16384.0)):
+        act(o, i, ACT.Copy, scale=c)
+    ts(v("Z1", 0, 144), v("q18"), pq, eq, 8192.0, mul)
+    act(v("t18"), v("t18"), ACT.Identity, scale=-1.0, bias=-14.5)
+    tt(v("Z2", 0, 144), v("Z1", 0, 144), v("t18"), mul)
+    act(v("Z1", 144, 288), v("Z1", 0, 144), ACT.Copy, scale=-1.0); act(v("Z2", 144, 288), v("Z2", 0, 144), ACT.Copy, scale=-1.0)
+    ms(v("Z1", 0, 144, 18), 0.0); ts(v("Z2", 0, 144, 18), q8, pq, eq, v("col", 16, 17), mul)
+    ms(v("ones"), 1.0)
+    cp(v("R0", 0, H), v("rp32", 0, H)); cp(v("R0", H, P), v("rp32", H, P))
+
+    def sel(name, r, lo=0):
+        return v(name, lo + 15 - r, lo + 143 - r)
+
+    big = [0, 0]
+
+    def bank(h):
+        big[h] += 1
+        return "p%d" % (2 * h + big[h] % 2)
+
+    def hv(name, h, n=H, lo=0, hi=None, st=1):
+        return v(name, h * n + lo, h * n + (n if hi is None else hi), st)
+
+    def near(h):
+        return [v("X%d" % h, c, c + H) for c in (0, 2 * H, H)]
+
+    def jumps(vis, h):
+        tag[1] = h
+        R, pv, ps, X = "R%d" % vis, "p%d" % (4 + h), "p%d" % (6 + h), Xs[h]
+        xk = lambda k: hv("x", h, 2048, k, None, 16)
+        for j in range(4):
+            gather(hv("x", h, 2048, 512 * j, 512 * j + 512), ind(X, hv(R, h, H, 32 * j, 32 * j + 32)))
+        for jj, ks in enumerate(([1, 2, 3, 4], [5, 6, 7], [8, 9, 10], [11, 12, 13])):
+            b = bank(h); k0 = ks[0]
+            mm([(v(b, H * j, H * j + H), [(Ib, xk(k + 1)), (nI, xk(k))]) for j, k in enumerate(ks)])
+            o, i = hv("ab", h, 13 * H, H * (k0 - 1), H * (k0 - 1 + len(ks))), v(b, 0, H * len(ks))
+            ak = lambda k: hv("ab", h, 13 * H, H * (k - 1), H * k)
+            if PAR["d"][2 * vis + h][jj] == "S":
+                act(o, i, ACT.Abs)
+                mm([(v(pv, k - 1, 104, 13), [(ak(k), b16)]) for k in ks])
+            else:
+                ts(o, i, 0.0, mxo)
+                mm([(v(pv, k - 1, 104, 13), [(ak(k), b32), (xk(k + 1), bm16), (xk(k), b16)]) for k in ks])
+        scan(hv("s1", h, 104), v("c1"), v(pv, 0, 104), addo, mxo)
+        ts(hv("ri", h, 8), hv("s1", h, 104, 12, None, 13), 15, band)
+        tt(hv("rT", h), ind(hv("ri", h, 8), bc16), v("db"), mul)
+        tt(hv("eqT", h), ind(hv("ri", h, 8), bc16), v("eqtab"), eq)
+        mm([(v(pv, 104, 128), [(hv("rT", h), v("L1", 0, 24)), (v("db"), v("L1", 24, 48))])])
+        mm([(v(ps, 0, MD * H), [(hv("eqT", h), v("II"))])])
+        cp(hv("pl", h, 24), v(pv, 104, 128))
+        gather(v(X[0], 0, XF), ind(hv("x", h, 2048), hv("pl", h, 24)))
+        act(hv("mask", h, MD * H), v(ps, 0, MD * H), ACT.Copy)
+        xp = near(h)[1]
+        mm([(v(pv, 128, 136), [(sel("Wsel", r, 144 * h), v(X[0], xp[1] + r, xp[2], 16)) for r in range(16)])])
+        cp(hv("ur", h, 8), v(pv, 128, 136))
+        ts(hv("u", h, 8), hv("ur", h, 8), W - 1, band)
+        tt(hv("uu", h, 8), hv("u", h, 8), hv("u", h, 8), mul)
+        tt(hv("z1", h, 144), ind(hv("u", h, 8), bcq), hv("KapT", h, 144), mul)
+        ts(hv("ua", h, 8), hv("uu", h, 8), 1.0 / 32, mul, v("Acol", vis, vis + 1), addo)
+        tt(hv("z2", h, 144), ind(hv("ua", h, 8), bcq), hv("z1", h, 144), addo)
+        ts(hv("CL", h, 144), hv("z2", h, 144), W - 1, band)
+        cp(hv("cl", h), ind(hv("CL", h, 144), perm))
+        m1 = hv("mask", h, MD * H, 0, H)
+        cp(hv("R16", h), hv(R, h))
+        ts(v("Q%d" % h, 0, H), hv(R, h), 262144.0, addo)
+        mm([(v(ps, 0, H), [(Ib, hv("R16", h)), (F1, m1)]),
+            (v(ps, 256, 384), [(nI, hv("R16", h)), (FA, m1), (FB, m1), (FC, m1), (FD, m1)])])
+        mm([(v(pv, 0, H), [(FE, m1)])])
+        act(hv("H0", h), v(ps, 0, H), ACT.Relu)
+        act(v(ps, 384, 512), v(ps, 256, 384), ACT.Relu, bias=4096.0)
+        tt(hv("Hh", h), hv("H0", h), v(pv, 0, H), addo)
+        ts(hv("u7", h, 8), hv("u", h, 8), 7, band)
+        tt(hv("n32", h, 8), hv("u7", h, 8), hv("NC", int(vis == TV - 1), 8), addo)
+        cp(hv("nl", h, 8), hv("n32", h, 8))
+
+    def sums(h):
+        tag[1] = h
+        for j in range(2):
+            part = lambda name: hv(name, h, K, 512 * j, 512 * j + 512)
+            cp(part("Q16"), part("Qk"))
+            b = bank(h)
+            mm([(v(b), [(sel("LBb", 0), part("Q16")), (sel("LBb", 1), part("Xk"))])])
+            act(part("Y"), v(b), ACT.Copy)
+
+    def stores(vis, h):
+        tag[1] = h
+        for name, tab, lo, src, lat in (("x", Xs[h], XF, "m2", 2400), ("q", Qs[h], H, "S2", 3000)):
+            cp(ind(tab, hv("nl", h, 8)), hv(src, h))
+            dma("Y", "e%s%d%d" % (name, vis, h), lambda a, t=tab[0], lo=lo: (T[t][rows(1 - a), lo + K * a:lo + K * a + K], T[t][rows(a), lo + K * a:lo + K * a + K]),
+                [tab], [tab], lat)
+            if vis == TV - 2:
+                k = name.upper() + "k"
+                dma("Y", "k%s%d" % (name, h), lambda a, t=tab[0], lo=lo, k=k: (T[k][rows(a), K * h:K * h + K], T[t][rows(a), lo + K * a:lo + K * a + K]),
+                    [hv(k, h, K)], [tab], lat)
+
+    def rivals(vis, h):
+        tag[1] = h
+        pv, X, Q = "p%d" % (4 + h), Xs[h], Qs[h]
+        for j in range(4):
+            gather(hv("Xc", h, 2048, 512 * j, 512 * j + 512), ind(X, hv("cl", h, H, 32 * j, 32 * j + 32)), 2.0)
+        for j in range(2):
+            for m in range(8 * j, 8 * j + 8, MD):
+                tt(hv("am", h, 2048, H * m, H * (m + MD)), ind(Q, hv("cl", h, H, 8 * m, 8 * (m + MD))), hv("mask", h, MD * H), mul)
+            mm([(v(pv, 136 + 64 * j, 200 + 64 * j), [(sel("Sel", r), hv("am", h, 2048, 1024 * j + r, 1024 * j + 1024, 16)) for r in range(16)])])
+            cp(hv("bl", h, H, 64 * j, 64 * j + 64), v(pv, 136 + 64 * j, 200 + 64 * j))
+            for i in range(2):
+                c = 64 * j + 32 * i
+                gather(hv("Xb", h, 2048, 16 * c, 16 * c + 512), ind(X, hv("bl", h, H, c, c + 32)))
+
+    def scores(vis, h):
+        tag[1] = h
+        pv = "p%d" % (4 + h)
+        xm, xp, x1 = near(h)
+        blocks = [[(0, v("I2"), xp, bm64, xm)]]
+        for j in range(4):
+            blocks.append([(m + 1, Ib, hv("Xc", h, 2048, H * m, H * m + H), bm32, hv("Xb", h, 2048, H * m, H * m + H)) for m in range(4 * j, 4 * j + 4)])
+        for j, bl in enumerate(blocks):
+            b = bank(h); n = H * len(bl); t0 = bl[0][0]
+            o = hv("mx", h, 17 * H, H * t0, H * t0 + n); ot = lambda t: hv("mx", h, 17 * H, H * t, H * t + H)
+            if PAR["e"][2 * vis + h][j] == "V":
+                mm([(v(b, H * i, H * i + H), [(l, c), (nI, x1)]) for i, (t, l, c, s, xb) in enumerate(bl)])
+                tt(o, v(b, 0, n), v(bl[0][4][0], bl[0][4][1], bl[0][4][1] + n), mxo)
+                mm([(v(pv, 288 + t, 432, 18), [(ot(t), b64), (c, s), (xb, bm32)]) for (t, l, c, s, xb) in bl])
+            else:
+                mm([(v(b, H * i, H * i + H), [(l, c), (nI, x1), (nI, xb)]) for i, (t, l, c, s, xb) in enumerate(bl)])
+                act(o, v(b, 0, n), ACT.Abs)
+                mm([(v(pv, 288 + t, 432, 18), [(ot(t), b32), (x1, bm32)]) for (t, l, c, s, xb) in bl])
+
+    def splice(vis, h):
+        tag[1] = h
+        pv = "p%d" % (4 + h)
+        scan(hv("s2", h, 144), v("c2"), v(pv, 288, 432), addo, mn)
+        ts(hv("twi", h, 8), hv("s2", h, 144, 17, None, 18), 31, band)
+        tt(hv("tT", h), ind(hv("twi", h, 8), bc16), v("db"), mul)
+        mm([(v(pv, 0, 288), [(hv("tT", h), v("Z1")), (v("db"), v("Z2"))])])
+        tt(hv("sb", h, 144), hv("CL", h, 144), v(pv, 0, 144), mn)
+        scan(hv("cwf", h, 144), v(pv, 144, 288), hv("sb", h, 144), mn, mxo)
+        won = hv("cwf", h, 144, 17, None, 18); cw = hv("cw", h, 8)
+        ts(cw, won, float(H), addo)
+        tt(hv("t1", h), ind(v("NUM"), cw), hv("Hh", h), mul)
+        ts(hv("t2", h), hv("t1", h), 1.0 / 32, mul, 8192 - 0.484375, addo)
+        tt(hv("t3", h), hv("t2", h), v("p%d" % (6 + h), 384, 512), sub)
+        tt(hv("t4", h), ind(v("Q%d" % h), cw), hv("t3", h), mxo)
+        ts(hv("S2", h), hv("t4", h), W - 1, band)
+        last = vis == TV - 1
+        src, dst = ("Of", "Rf") if last else ("O%d" % vis, "R%d" % (vis + 1))
+        cp(hv(src, h), hv("S2", h))
+        s = add("G", [lambda q: send(q, ap(hv(dst, h)), ap(hv(src, h)), "ar%d%d" % (vis, h), last)], [], [hv(src, h)], 500.0, remote=True)
+        add("N", [], [hv(dst, h)], [], 0.0, sem="ar%d%d" % (vis, h), lat=COST["LINK"], after=s, last=last)
+        tt(hv("m1", h), ind(v("X%d" % h, XF - H), cw), near(h)[2], addo)
+        if not last:
+            ts(hv("m2", h), hv("m1", h), 0.5, mul, -0.25, addo)
+            act(hv("sg", h, 8), won, ACT.Sign, bias=0.5)
+        else:
+            ts(hv("m16", h), hv("m1", h), 0.5, mul, 1023.75, addo)
+            b = bank(h); Y = hv("Y", h, K)
+            mm([(v(b, 0, H), [(sel("LBf", 0), hv("Of", h)), (sel("LBb", 1), hv("m16", h))])])
+            act(hv("ys", h), v(b, 0, H), ACT.Identity, bias=yb)
+            cp(ind(Y, hv("nl", h, 8)), hv("ys", h))
+            dma("Y", "oq%d" % h, lambda a: (T.yq[4 * h:4 * h + 4, K * a:K * a + K], T.Y[64 * a:64 * a + 64:16, K * h:K * h + K]), [], [Y], 2000)
+            dma("YS"[h], "ox%d" % h, lambda a: (T.yx[4 * h:4 * h + 4, K * a:K * a + K], T.Y[64 * a + 1:64 * a + 64:16, K * h:K * h + K]), [], [Y], 2000)
+            dma("Y", "or%d" % h, lambda a: (T.yr[rows(h), H * a:H * a + H], T.Rf[rows(a), H * h:H * h + H]), [], [hv("Rf", h)], 2000)
+
+    for vis in range(TV):
+        for h in range(2):
+            jumps(vis, h)
+            if vis == TV - 1:
+                sums(h)
+            rivals(vis, h); scores(vis, h); splice(vis, h)
+            if vis < TV - 1:
+                stores(vis, h)
+        if vis < TV - 1:
+            b = bank(1)
+            mm([(v(b, 0, 16), [(v("ones"), v("sg"))])])
+            act(v("aj"), v(b, 0, 16), ACT.Identity, bias=64 - 0.484375 / 16, scale=0.5, acc=v("Acol", vis + 1, vis + 2))
+    return ops
+
+
+def depend(ops):
+    seen = {}
+    for i, o in enumerate(ops):
+        dep = set()
+        for acc, wr in ((o["r"], False), (o["w"], True)):
+            for (name, lo, hi, st) in acc:
+                ps = SCRATCH[name][0] == "psum"
+                for (j, l2, h2, w2) in seen.get(name, []):
+                    if j != i and ((l2 < hi and lo < h2 and (wr or w2)) or (ps and ops[j]["eng"] != o["eng"])):
+                        dep.add(j)
+        for acc, wr in ((o["r"], False), (o["w"], True)):
+            for (name, lo, hi, st) in acc:
+                seen.setdefault(name, []).append((i, lo, hi, wr))
+        o["dep"] = dep; o["id"] = i
+        o["sdep"] = dep | ({o["after"]["id"]} if "after" in o else set())
+    anc = []
+    for o in ops:
+        a = 0
+        for j in o["sdep"]:
+            a |= anc[j]
+        o["sdep"] = {j for j in o["sdep"] if not (a >> j) & 1 or ops[j].get("lat")}
+        for j in o["sdep"]:
+            a |= 1 << j
+        anc.append(a)
+
+
+def order(ops):
+    HOP, SAME = COST["HOP"], COST["SAME"]
+    succ = [[] for _ in ops]
+    for o in ops:
+        for j in o["sdep"]:
+            succ[j].append(o["id"])
+    prio = [0.0] * len(ops)
+    for o in reversed(ops):
+        prio[o["id"]] = o["cost"] + o.get("lat", 0) + max([prio[j] + HOP for j in succ[o["id"]]], default=0.0)
+    prio = [p + PAR["lead"] * (1 - o["half"]) + 100.0 * PAR["bias"].get("%s.%d" % (o["w"] or o["r"])[0][:2], 0) for p, o in zip(prio, ops)]
+    free = {e: 0.0 for e in "VSPGYN"}
+    left = [len(o["sdep"]) for o in ops]; rdy = [0.0] * len(ops); fin = [0.0] * len(ops)
+    pool = [o["id"] for o in ops if not o["sdep"]]; seq = []
+    while pool:
+        best = min(pool, key=lambda i: (max(rdy[i], free[ops[i]["eng"]]), -prio[i]))
+        e = ops[best]["eng"]; t0 = max(rdy[best], free[e])
+        i = max((i for i in pool if ops[i]["eng"] == e and rdy[i] <= t0 + PAR["look"]), key=lambda i: prio[i])
+        o = ops[i]; t0 = max(rdy[i], free[e])
+        free[e] = t0 + o["cost"]; fin[i] = free[e] + o.get("lat", 0); o["t0"] = t0
+        pool.remove(i); seq.append(i)
+        for j in succ[i]:
+            rdy[j] = max(rdy[j], fin[i] + (SAME if ops[j]["eng"] == e else HOP)); left[j] -= 1
+            if left[j] == 0:
+                pool.append(j)
+    return seq, max(fin)
+
+
+def place(ops, key, pred, succ, back):
+    left = [len(p) for p in pred]; st = [0.0] * len(ops); done = [0.0] * len(ops); eng = [None] * len(ops)
+    busy = {e: [] for e in "VSPGYN"}
+    pool = [i for i in range(len(ops)) if not left[i]]
+    while pool:
+        i = min(pool, key=lambda j: (key[j], j)); pool.remove(i)
+        o = ops[i]; best = None
+        for e, (_, cost) in o.get("opt", {o["eng"]: (None, o["cost"])}).items():
+            t = o.get("lat", 0) if back else 0.0
+            for j in pred[i]:
+                t = max(t, done[j] + (COST["SAME"] if eng[j] == e else COST["HOP"]) + (o if back else ops[j]).get("lat", 0))
+            gaps = busy[e]; k = len(gaps)
+            while k and gaps[k - 1][1] > t:
+                k -= 1
+            while k < len(gaps) and t + cost > gaps[k][0]:
+                t = max(t, gaps[k][1]); k += 1
+            mark = t + cost + (PAR["vpen"] if e == "V" else 0.0)
+            if best is None or mark < best[0]:
+                best = (mark, e, k, t, cost)
+        _, e, k, t, cost = best
+        busy[e].insert(k, (t, t + cost)); st[i] = t; done[i] = t + cost; eng[i] = e
+        for j in succ[i]:
+            left[j] -= 1
+            if not left[j]:
+                pool.append(j)
+    return st, done, eng
+
+
+def refine(ops):
+    pred = [sorted(o["sdep"]) for o in ops]; succ = [[] for _ in ops]
+    for o in ops:
+        for j in pred[o["id"]]:
+            succ[j].append(o["id"])
+    if PAR["key"] is None:
+        order(ops)
+    key = PAR["key"] or [o["t0"] for o in ops]; best = None
+    for n in range(PAR["rounds"]):
+        st, done, eng = place(ops, key, pred, succ, False)
+        end = max(d + o.get("lat", 0) for d, o in zip(done, ops))
+        if best is None or end < best[0]:
+            best = (end, st, eng)
+        if n + 1 < PAR["rounds"]:
+            key = [-d for d in place(ops, [-d for d in done], succ, pred, True)[1]]
+    for o, t, e in zip(ops, best[1], best[2]):
+        o["t0"] = t
+        if "opt" in o:
+            o["eng"] = e; o["fns"], o["cost"] = o["opt"][e]
+    return sorted(range(len(ops)), key=lambda i: (best[1][i], i)), best[0]
+
+
+def rank_program(g, core, T, topo):
+    rank = T.rank_of(core)
+    if rank is None:
+        return
+    cores = list(T.cores); n = len(cores)
+
+    def lanes(src, dst):
+        return topo.engines(src, dst)[:8]
+
+    def peer(last, sign):
+        return cores[(rank + sign * (-(TV - 1) if last else 1)) % n]
+
+    sent = [0]
+
+    def send(q, out_ap, in_ap, sem, last):
+        d = peer(last, 1); rid, pid = topo.addr(d, core); es = lanes(core, d)
+        q.remote_dma(out_ap, in_ap, T.sem[sem], T.sem["sent"], pid, rid, sum(1 << e for e in es))
+        sent[0] += len(es)
+
+    ops = build(T, send)
+    depend(ops)
+    seq, _ = refine(ops)
+    queue = {"V": g.vector, "S": g.scalar, "P": g.tensor, "G": g, "Y": g.sync}
+    count = {e: 0 for e in "VSPG"}; known = {e: {} for e in "VSPGY"}; total = {}
+    for i in seq:
+        o = ops[i]; e = o["eng"]
+        if e == "N":
+            o["tok"] = (o["sem"], len(lanes(peer(o["last"], -1), core))); o["know"] = {}
+            total[o["sem"]] = o["tok"][1]
+            continue
+        q, kn = queue[e], known[e]
+        for d in sorted((ops[j] for j in o["dep"] if "tok" in ops[j]), key=lambda d: -d["t0"]):
+            s, c = d["tok"]
+            if kn.get(s, 0) < c:
+                q.wait_ge(T.sem[s], c); kn[s] = c
+                for s2, c2 in d["know"].items():
+                    kn[s2] = max(kn.get(s2, 0), c2)
+        o["know"] = dict(kn)
+        if o.get("remote"):
+            o["fns"][0](q)
+        elif "sem" in o:
+            for f in o["fns"]:
+                f(q).then_inc(T.sem[o["sem"]], 16)
+            o["tok"] = (o["sem"], 16 * len(o["fns"])); total[o["sem"]] = o["tok"][1]
+        else:
+            for f in o["fns"]:
+                f(q).then_inc(T.sem["c" + e], 1); count[e] += 1
+            o["tok"] = ("c" + e, count[e]); total["c" + e] = count[e]
+    total["sent"] = sent[0]
+    for s, c in total.items():
+        g.wait_ge(T.sem[s], c)

@@ -1,69 +1,88 @@
-import numpy as np
+import math
 from concourse.mybir import AluOpType, ActivationFunctionType
 
 ALU = AluOpType
 ACT = ActivationFunctionType
 W, P, TV, H = 2048, 256, 3, 128
-XF = 3 * H
-MD = 2
+MD = 4
+XW = W + 16
 F32, BF, F16, I32, U16 = "float32", "bfloat16", "float16", "int32", "uint16"
 
 SCRATCH = {
-    "X0": ("sbuf", [128, XF + W], BF), "X1": ("sbuf", [128, XF + W], BF), "Q0": ("sbuf", [128, H + W], I32), "Q1": ("sbuf", [128, H + W], I32),
-    "NUM": ("sbuf", [128, H + W], F32), "Y": ("sbuf", [128, W], F32), "Q16": ("sbuf", [128, W], F16),
-    "Qk": ("sbuf", [128, W], I32), "Xk": ("sbuf", [128, W], BF),
-    "x": ("sbuf", [128, 4096], BF), "ab": ("sbuf", [128, 2 * 13 * H], BF), "am": ("sbuf", [128, 4096], F16),
-    "Xc": ("sbuf", [128, 4096], BF), "Xb": ("sbuf", [128, 4096], BF), "mx": ("sbuf", [128, 2 * 17 * H], F16),
+    "X0": ("sbuf", [128, W + 10 * H], BF), "X1": ("sbuf", [128, W + 10 * H], BF),
+    "Q0": ("sbuf", [128, W + H], I32), "Q1": ("sbuf", [128, W + H], I32),
+    "NUM": ("sbuf", [128, W + H], F32), "Y": ("sbuf", [128, 2 * W], F32), "Q16": ("sbuf", [128, W], F16), "Yc": ("sbuf", [128, P], F32),
+    "x": ("sbuf", [128, 16 + 2 * XW], BF), "ab": ("sbuf", [128, 2 * 13 * H], BF), "am": ("sbuf", [128, 4096], F16),
+    "Xc": ("sbuf", [128, 4096], BF), "Xb": ("sbuf", [128, 4096], F16), "mx": ("sbuf", [128, 2 * 17 * H], F16),
     "rp32": ("sbuf", [128, P], I32), "R0": ("sbuf", [128, P], U16), "R1": ("sbuf", [128, P], U16), "R2": ("sbuf", [128, P], U16),
     "O0": ("sbuf", [128, P], U16), "O1": ("sbuf", [128, P], U16), "Of": ("sbuf", [128, P], F32), "Rf": ("sbuf", [128, P], F32),
     "R16": ("sbuf", [128, P], F16), "s1": ("sbuf", [128, 208], I32), "ri": ("sbuf", [128, 16], I32),
-    "eqT": ("sbuf", [128, P], BF), "rT": ("sbuf", [128, P], BF), "mask": ("sbuf", [128, 2 * MD * H], BF), "pl": ("sbuf", [128, 48], U16),
-    "ur": ("sbuf", [128, 16], I32), "u": ("sbuf", [128, 16], I32), "uu": ("sbuf", [128, 16], F32), "ua": ("sbuf", [128, 16], I32),
-    "z1": ("sbuf", [128, 288], F32), "z2": ("sbuf", [128, 288], I32), "CL": ("sbuf", [128, 288], I32), "cl": ("sbuf", [128, P], U16),
-    "bl": ("sbuf", [128, P], U16), "H0": ("sbuf", [128, P], F32), "Hh": ("sbuf", [128, P], F32),
-    "s2": ("sbuf", [128, 288], I32), "twi": ("sbuf", [128, 16], I32), "tT": ("sbuf", [128, P], BF),
-    "sb": ("sbuf", [128, 288], F32), "cwf": ("sbuf", [128, 288], F32), "cw": ("sbuf", [128, 16], U16),
-    "t1": ("sbuf", [128, P], F32), "t2": ("sbuf", [128, P], I32), "t3": ("sbuf", [128, P], F32), "t4": ("sbuf", [128, P], I32),
+    "ut": ("sbuf", [128, 16], I32), "uT": ("sbuf", [128, P], F16), "q8e": ("sbuf", [128, 8], BF),
+    "rT": ("sbuf", [128, P], BF), "pl": ("sbuf", [128, 64], U16),
+    "ur": ("sbuf", [128, 16], I32), "u": ("sbuf", [128, 16], I32), "uu": ("sbuf", [128, 16], F32),
+    "z1": ("sbuf", [128, 320], I32), "z2": ("sbuf", [128, 320], I32), "CL": ("sbuf", [128, 320], I32), "cl": ("sbuf", [128, 288], U16),
+    "bl": ("sbuf", [128, P], U16), "Hh": ("sbuf", [128, P], F32),
+    "s2": ("sbuf", [128, 272], I32), "twi": ("sbuf", [128, 16], I32), "tT": ("sbuf", [128, P], BF),
+    "cwf": ("sbuf", [128, 288], I32), "cwi": ("sbuf", [128, 16], I32), "cw": ("sbuf", [128, 16], U16),
+    "Qw": ("sbuf", [128, P], F32), "t1": ("sbuf", [128, P], F32), "t3": ("sbuf", [128, P], I32), "t4": ("sbuf", [128, P], I32),
     "S2": ("sbuf", [128, P], I32), "m1": ("sbuf", [128, P], F16), "m2": ("sbuf", [128, P], I32), "m16": ("sbuf", [128, P], F16),
-    "ys": ("sbuf", [128, P], F32), "u7": ("sbuf", [128, 16], I32), "n32": ("sbuf", [128, 16], I32), "nl": ("sbuf", [128, 16], U16),
-    "sg": ("sbuf", [128, 16], BF), "aj": ("sbuf", [128, 16], F32), "Acol": ("sbuf", [128, 4], F32),
+    "ys": ("sbuf", [128, P], F32), "sg": ("sbuf", [128, 16], BF), "aj": ("sbuf", [128, 16], F32), "Acol": ("sbuf", [128, 4], F32),
     "wk": ("sbuf", [128, 16], I32), "col": ("sbuf", [128, 24], F32), "pI": ("sbuf", [128, 8], I32),
     "D0": ("sbuf", [128, 128], F32), "KK": ("sbuf", [128, 128], BF), "G16": ("sbuf", [128, 128], BF), "C144": ("sbuf", [128, 144], BF),
-    "q18": ("sbuf", [128, 144], BF), "t18": ("sbuf", [128, 144], BF), "sm": ("sbuf", [128, 128], F32), "smi": ("sbuf", [128, 16], I32),
-    "II": ("sbuf", [128, MD * 128], BF), "nI": ("sbuf", [128, 128], BF), "I2": ("sbuf", [128, 128], BF), "BLK": ("sbuf", [128, 128], BF),
-    "ones": ("sbuf", [128, 128], BF), "b8": ("sbuf", [128, 48], BF),
+    "t18": ("sbuf", [128, 144], BF), "q18": ("sbuf", [128, 144], BF), "e18": ("sbuf", [128, 432], BF), "sm": ("sbuf", [128, 128], F32), "smi": ("sbuf", [128, 16], I32),
+    "Ib": ("sbuf", [128, 128], BF), "nI": ("sbuf", [128, 128], BF), "I32": ("sbuf", [128, 128], BF), "BLK": ("sbuf", [128, 128], BF),
+    "ones": ("sbuf", [128, 128], BF), "I2": ("sbuf", [128, 128], BF), "b8": ("sbuf", [128, 48], BF),
     "Sel": ("sbuf", [128, 144], BF), "Wsel": ("sbuf", [128, 288], BF), "LBb": ("sbuf", [128, 144], BF),
-    "LBf": ("sbuf", [128, 144], F32), "db": ("sbuf", [128, 128], BF), "eqtab": ("sbuf", [128, 128], BF),
-    "L1": ("sbuf", [128, 48], F16), "Z1": ("sbuf", [128, 288], BF), "Z2": ("sbuf", [128, 288], BF), "kd": ("sbuf", [128, 288], F16),
-    "KapT": ("sbuf", [128, 288], F32), "NC": ("sbuf", [128, 16], F32), "lists": ("sbuf", [128, 32], U16),
-    "c1": ("sbuf", [128, 104], F32), "c2": ("sbuf", [128, 144], F32), "tm": ("sbuf", [128, 32], F32), "tb": ("sbuf", [128, 640], BF),
-    "F": ("sbuf", [128, 768], BF),
+    "LBf": ("sbuf", [128, 144], F32), "LBa": ("sbuf", [128, 288], BF), "db": ("sbuf", [128, 128], BF),
+    "L1": ("sbuf", [128, 64], F16), "Z1": ("sbuf", [128, 144], BF), "Z2": ("sbuf", [128, 144], BF), "Z3": ("sbuf", [128, 8], BF),
+    "kd": ("sbuf", [128, 288], F16), "KapT": ("sbuf", [128, 288], F32), "lists": ("sbuf", [128, 32], U16),
+    "c1": ("sbuf", [128, 104], F32), "c2": ("sbuf", [128, 136], F32), "zc": ("sbuf", [128, 160], F32), "tm": ("sbuf", [128, 16], F32),
+    "FH": ("sbuf", [128, 128], BF), "FW": ("sbuf", [128, 128], F16), "Ff": ("sbuf", [128, 128], F32),
 }
 for _b in range(8):
-    SCRATCH["p%d" % _b] = ("psum", [128, 512], F32)
-DMAS = [a + str(h) for a in ("lx", "lr", "lq", "lw", "lk", "oq", "ox", "or", "kq", "kx", "ex0", "ex1", "eq0", "eq1") for h in range(2)]
+    SCRATCH["p%d" % _b] = ("psum", [128, 32, 16] if _b < 4 else [128, 512], F32)
+DMAS = [a + str(h) for a in ("lx", "lr", "lq", "lw", "lk", "oq", "ox", "or", "yc", "ex0", "ex1", "eq0", "eq1") for h in range(2)]
 SEMAPHORES = ["cV", "cS", "cP", "cG", "sent"] + DMAS + ["ar%d%d" % (v, h) for v in range(TV) for h in range(2)]
 
-COST = {"CY": 1.04, "GA": 1.55, "SC": 3.5, "PE": 0.52, "TT2": 1.0, "HOP": 120.0, "SAME": 70.0, "LINK": 2600.0, "TG": 0.0}
+COST = {"CY": 1.0, "GA": 1.5, "SC": 3.5, "PE": 0.5, "PF": 0.0, "TT2": 1.0, "HOP": 120.0, "SAME": 70.0, "LINK": 2800.0, "GX": 1.5, "GA0": 100.0, "FIRST": 3000.0}
 WIDTH = {F32: 4, I32: 4, BF: 2, F16: 2, U16: 2}
-PAR = {"d": ["SSSS"] * 6, "e": ['SVVVS', 'SVVSV', 'SSVSV', 'SVSVV', 'SVVVS', 'SVVVS'], "lead": 5000.0, "look": 100.0, "bias": {}, "rounds": 1, "vpen": 300.0}
-KEY = "0g060v0t1o1r1p17191f0201080a131512362u10295v50143c1c0s11240x0z0y161a1l5d5wjt1j30331ik70i221kk6282i3d5y2d3v2q1n2p2o2n2r39egjf253a3e183m0r2f1z1v311u1m1w261y5jiv03090k070b0j0d0e0p0f0m20211t1h544z4n7k000o0h0c04050l0q1d0n0u2a1s1x2b1b1g1q231e2e2t2h2v2z2w3h323l2l2j270w2g3g3j3q493w463x5x486k6r6w3y3o444r3p3t2x38474e4m4j4d4f4h4l4s4x5a534342574g4o5851555h5c5g5m5f5k5o5q5r5t6266696b6d6g6l6q6t6v6z706h6m8q6y728e8r2m2k2c2s2y3b3s353f3u3i3k3z3r3n343740414a4b4q4c454i4k4p4t4v4u4w4y5259567h5u645z7t617y828m5s5n60675b5l5e5i656a6e6p63686c5p6o6s6u776f6j736i6n716x757b74797c787a7d7f7g7j7m7o7p767s7u7w7x8184878d7r8397808c86al8x927i7n7l7q7v7e8g7z898j8b85888a8h8i8l8n8p8w8o8y8s8u969093958f94989a9b9d9ca98z9h8kbg9mc1bvbma69iah9v9j9g9l9t9za39sab9q9r9xa2adanaqb29f9naxapazbaaearbeb7bdbib4akb5blbpbrc0c5c8cfcdcgciclckcacbchc2cnedcscvdycucxde8t918v999e9pa19k9oa49wa0a59u9ya7a8aaacafajb3agaib9asauavayawb6aob8amb1d2atbkbhd8bqdwdsdvbsbococcbbbfbjbnbtbwbxc4bubyc3c6cjcmcqd4bcb0crbzc7cwc9cecyctczd0cpd1d3d5d6d7dddfdhdjdidkdodrdue8eaeidze9ebe7ehfve1dmeke6efdad9e3dpdxe4eje5dle0dndtdgdqdce2eldbeeeoeqepeteuereyf2f5f7f8fcfbfjfmevipf0f3f6ilf9jljnjremesenecexfaftfxg0gafpfsfufng1g6gggjfwfzg4gcgmgph2grfffkhfgfgnhggigshmgvguhdh3h9hpi1i2i8iaj7iyj0j2jdjgiwjojqjyjuk0k4k2k5k3jvjzjwewf1ezf4feflg3fdfgfyfhfrg2fofqg5g7g9gbgdgkgoglg8gtgwh0gxgzh1h4hcgyh8h6iqhehshij4hvjpjsk1figegqghhbhthjhuhni0hkhhh7hlhyi3i5hqhohrhwhzi6ibijidh5haiehxiciii4ihirifiojeiniti7i9ixigikimiuj6j8jaisizj1j3j5jbjijjjkjmjhjcjxj9"
-PAR["key"] = [int(KEY[_i:_i + 2], 36) for _i in range(0, len(KEY), 2)]
+PAR = {"t4": 0, "ut": 0, "n3": 0, "dq": 1, "de": 1, "os": 1, "su": 1, "num": 1024, "b": ["VVVV"] * 6, "jb": 3, "ns": 2, "nx": 4, "nc": 4, "sint": 1, "m1": "V", "walk": 1, "look": 310.0, "fill": 120.0, "dup": "GG",
+       "rounds": 1, "vpen": 100.0, "key": None}
+PAR["lead"] = {'x00': 39, 'j00': 185, 'a00': 89, 'p00': -95, 'r00': 36, 'e00': 65, 'w00': 44, 's00': -14, 'x01': -38, 'j01': -21, 'a01': 5, 'p01': -224, 'r01': 0, 'e01': -2, 'w01': 28, 's01': 39, 'x10': 41, 'j10': 43, 'a10': 103, 'p10': -112, 'r10': 11, 'e10': 39, 'w10': 19, 's10': -14, 'x11': 27, 'j11': 44, 'a11': -5, 'p11': -104, 'r11': -11, 'e11': -61, 'w11': -129, 's11': -115, 'x20': 85, 'j20': 103, 'a20': 119, 'p20': -16, 'r20': 64, 'e20': 18, 'w20': 55, 's20': -147, 'x21': 0, 'j21': 15, 'a21': 86, 'p21': -204, 'r21': 2, 'e21': 3, 'w21': 103, 's21': -50, 'g00': 44, 'c00': 114, 'y20': -181, 'y21': -40}
+PAR.update(look=350.0, fill=150.0, vpen=100.0, num=2048, n3=0, dq=0, de=0, os=0, su=0, nc=4, jb=3, ns=2, m1="S", ut=0, b=["SSSS"] * 6, t4=1)
+PAR.update(aim=0.4, fx=0, steps=110000, heat=0.0003, seed=1, nc=2, su=0, num=2048)
+PAR["lead"] = dict({p + str(v) + "0": 40 for v in range(TV) for p in "xjapyrews"}, g00=60, c00=150)
+COST.update(CY=1.0, GA=1.5, SC=3.5, PE=.5, PF=0.0, PM=64, HOP=120., SAME=70., LINK=2600., FIRST=500., GX=1.4, GA0=80., TG=0.0, SF=0.0, SX=1.0,
+            SEND=500.0, ISSUE=60.0, WAKE=200.0, D0=1200.0, D1=700.0, RATE=400.0)
+SIZE = {"lx": 512, "lq": 1024, "lr": 64, "lw": 8, "lk": 8, "ex": 256, "eq": 512, "yc": 64, "oq": 32, "ox": 32, "or": 64}
+GUESS = [dict(CY=1.04, GA=1.55, PE=.52, GX=1.3, GA0=0.0),
+         dict(CY=1.01, GA=1.27, PE=.45, SAME=50., LINK=1700., SEND=200., SF=22., SX=1.12, TG=2.0, TT2=2.0, RATE=600., GX=1.2, GA0=0.0),
+         dict(CY=.95, GA=1.57, PE=.4, SAME=160., LINK=1500., SF=40., SX=1.12, WAKE=0.0, RATE=490., D1=400., GX=1.0, GA0=0.0),
+         dict(CY=.93, GA=1.6, SC=2.8, PE=.47, PF=5., HOP=70., SAME=110., LINK=3200., SEND=1000., FIRST=1500., SF=40., TG=2.0, RATE=330., D0=1600.,
+              GX=1.6, GA0=0.0),
+         dict(CY=.92, GA=1.35, SC=3.5, PE=.76, HOP=110., SAME=80., LINK=2200., SEND=500., FIRST=800., SF=30., TG=1.8, RATE=450., D0=1300.,
+              WAKE=300., GX=1.4, GA0=0.0)]
 
 
 def build(T, send):
     ops = []
     CY, GA, SC, PE = COST["CY"], COST["GA"], COST["SC"], COST["PE"]
-    tag = [0, 0]
+    tag = [0, 0, "c"]
 
-    def v(name, lo=0, hi=None, st=1):
-        return (name, lo, SCRATCH[name][1][1] if hi is None else hi, st)
+    def v(name, lo=0, hi=None, st=1, a=None):
+        return (name, lo, SCRATCH[name][1][1] if hi is None else hi, st, a)
+
+    def rows(a):
+        return slice(0, 128) if a is None else slice(64 * a, 64 * a + 64)
 
     def ap(a):
         if isinstance(a, tuple) and a[0] == "ind":
             return ap(a[1]).indirect(ap(a[2]))
+        if isinstance(a, tuple) and len(SCRATCH[a[0]][1]) == 3:
+            k = a[1] % 16 if a[3] == 16 else slice(*a[5]) if len(a) > 5 else slice(0, 16)
+            return T[a[0]][:, a[1] // 16:a[2] // 16, k]
         if isinstance(a, tuple):
-            return T[a[0]][:, a[1]:a[2]:a[3]] if a[3] != 1 else T[a[0]][:, a[1]:a[2]]
+            return T[a[0]][rows(a[4]), a[1]:a[2]:a[3]] if a[3] != 1 else T[a[0]][rows(a[4]), a[1]:a[2]]
         return a
 
     def ind(win, off):
@@ -79,6 +98,8 @@ def build(T, send):
     def n_of(a):
         if a[0] == "ind":
             return 16 * (a[2][2] - a[2][1])
+        if len(a) > 5:
+            return (a[2] - a[1]) // 16 * (a[5][1] - a[5][0])
         return (a[2] - a[1] + a[3] - 1) // a[3]
 
     def add(eng, fns, outs, ins, cost, **kw):
@@ -88,7 +109,7 @@ def build(T, send):
                 w.append(o[1]); r.append(o[2])
             else:
                 w.append(o)
-        d = {"eng": eng, "fns": fns, "w": w, "r": r, "cost": cost, "half": tag[1]}
+        d = {"eng": eng, "fns": fns, "w": w, "r": r, "cost": cost, "vis": tag[0], "half": tag[1], "ph": tag[2]}
         d.update(kw)
         ops.append(d)
         return d
@@ -96,9 +117,9 @@ def build(T, send):
     def vcost(out, ins, tt=False):
         n = n_of(out)
         if out[0] == "ind":
-            return 50 + n * SC * CY
+            return 50 + 16 * (out[2][2] - out[2][1]) * SC * CY
         if ins[0][0] == "ind":
-            return 50 + n * max(GA, COST["TG"] if tt else 0.0) * CY
+            return 50 + n * max(GA, COST.get("TG", 0) if tt else 0) * CY
         two = all(WIDTH[SCRATCH[a[0]][2]] == 2 for a in views([out] + ins))
         c = 1.0
         if tt and not any(SCRATCH[a[0]][0] == "psum" for a in views(ins)):
@@ -133,7 +154,8 @@ def build(T, send):
         if acc is not None: kw["accum_out"] = acc
         f = lambda q: q.activation(ap(out), ap(in_), func, **{k: ap(a) for k, a in kw.items()})
         n = n_of(out)
-        return add("S", [f], [out] + ([acc] if acc else []), [in_, bias, scale], 65 + n * GA * CY if in_[0] == "ind" else max(64, n) * CY)
+        return add("S", [f], [out] + ([acc] if acc else []), [in_, bias, scale],
+                   COST.get("SF", 0) + (65 + n * GA * CY * COST.get("SG", 1) if in_[0] == "ind" else max(64, n) * CY * COST.get("SX", 1)))
 
     def gather(out, in_, scale=None):
         a = cp(out, in_) if scale is None else ts(out, in_, scale, ALU.mult)
@@ -142,69 +164,85 @@ def build(T, send):
         b["opt"] = {"S": (b["fns"], b["cost"]), "V": (a["fns"], a["cost"])}
         return b
 
-    def mm(groups):
+    def affine(out, in_, scale, bias):
+        a = ts(out, in_, scale, ALU.mult, bias, ALU.add)
+        if not PAR["sint"]:
+            return a
+        ops.pop()
+        b = act(out, in_, ACT.Identity, scale=scale, bias=bias)
+        b["opt"] = {"S": (b["fns"], b["cost"]), "V": (a["fns"], a["cost"])}
+        return b
+
+    def mm(groups, first=True, last=True):
         fns, outs, ins, cost = [], [], [], 0.0
         for out, terms in groups:
             outs.append(out)
-            for i, (l, r) in enumerate(terms):
-                fns.append(lambda q, o=out, l=l, r=r, a=(i == 0), z=(i == len(terms) - 1): q.matmul(ap(o), ap(l), ap(r), a, z))
+            for i, t in enumerate(terms):
+                l, r, o = t[0], t[1], t[2] if len(t) > 2 else out
+                fns.append(lambda q, o=o, l=l, r=r, a=(first and i == 0), z=(last and i == len(terms) - 1): q.matmul(ap(o), ap(l), ap(r), a, z))
                 ins += [l, r]
-                cost += max(64, n_of(r)) * PE * (4 if SCRATCH[l[0]][2] == F32 else 1)
-        return add("P", fns, outs, ins, cost)
+                cost += COST.get("PF", 0) + max(min(COST.get("PM", 64), n_of(l)), n_of(r)) * PE * (4 if SCRATCH[l[0]][2] == F32 else 1)
+        return add("P", fns, outs, ins, cost, goes_on=not first)
 
     def iota(out, pattern, base, cm):
         if SCRATCH[out[0]][2] == I32:
             f = lambda q: q.iota(ap(out), pattern, base, cm)
         else:
             f = lambda q: q.iota(ap(out), pattern, base, cm, allow_small_or_imprecise_dtypes=True)
-        return add("G", [f], [out], [], 130 + 2 * n_of(out) * CY)
+        return add("G", [f], [out], [], COST["GX"] * (130 + 2 * n_of(out) * CY) + COST["GA0"])
 
-    def keep(out, in_, op, base, sign):
-        return add("G", [lambda q: q.affine_select(ap(out), ap(in_), [[sign, 128]], op, 0.0, base, -sign)], [out], [in_], 170 + 256 * CY)
+    def keep(out, in_, pattern, op, fill, base, cm):
+        return add("G", [lambda q: q.affine_select(ap(out), ap(in_), pattern, op, fill, base, cm)], [out], [in_],
+                   COST["GX"] * (170 + 2 * n_of(out) * CY) + COST["GA0"])
 
-    def dma(eng, sem, f, outs, ins, lat):
-        return add(eng, [lambda q, a=a: q.dma_start(*f(a)) for a in range(2)], outs, ins, 120.0, sem=sem, lat=lat)
+    def gcopy(out, in_):
+        return keep(out, in_, [[0, n_of(out)]], ALU.is_ge, 0.0, 0, 0)
 
-    eq, mul, sub, addo, mn, mxo, band = ALU.is_equal, ALU.mult, ALU.subtract, ALU.add, ALU.min, ALU.max, ALU.bitwise_and
-    Xs, Qs = [v("X%d" % h, XF) for h in range(2)], [v("Q%d" % h, H) for h in range(2)]
+    def dma(eng, sem, f, outs, ins, lat, n=2):
+        return add(eng, [lambda q, a=a: q.dma_start(*f(a)) for a in range(n)], outs, ins, COST["ISSUE"] * n, sem=sem, lat=lat,
+                   bytes=1024 * SIZE[sem[:2]], load=sem[0] == "l")
+
+    eq, ne, ge, mul, sub, addo, mn, mxo, band = (ALU.is_equal, ALU.not_equal, ALU.is_ge, ALU.mult, ALU.subtract, ALU.add, ALU.min, ALU.max,
+                                                 ALU.bitwise_and)
+    shr = ALU.arith_shift_right
+    Xs, Qs = [v("X%d" % h, 0, W) for h in range(2)], [v("Q%d" % h, 0, W) for h in range(2)]
     K = W // 2
 
-    def rows(a):
-        return slice(64 * a, 64 * a + 64)
+    def hv(name, h, n=H, lo=0, hi=None, st=1, a=None):
+        return v(name, h * n + lo, h * n + (n if hi is None else hi), st, a)
+
+    def xv(h, lo, hi, st=1):
+        return v("x", 16 + XW * h + lo, 16 + XW * h + hi, st)
 
     for h in range(2):
         dma("S", "lr%d" % h, lambda a, h=h: (T.rp32[rows(a), H * h:H * h + H], T.rp[rows(h), H * a:H * a + H]), [v("rp32", H * h, H * h + H)], [], 2200)
-        dma("Y", "lx%d" % h, lambda a, h=h: (T["X%d" % h][rows(a), XF:], T.xf[rows(h), :]), [Xs[h]], [], 3200 + 1800 * h)
+        dma("Y", "lx%d" % h, lambda a, h=h: (T["X%d" % h][rows(a), 0:W], T.xf[rows(h), :]), [Xs[h]], [], 3200 + 1800 * h)
     for h in range(2):
         dma("Y", "lw%d" % h, lambda a, h=h: (T.wk[rows(a), 4 * h:4 * h + 1], T.wt[rows(h), :]), [v("wk", 4 * h, 4 * h + 4)], [], 5000)
         dma("Y", "lk%d" % h, lambda a, h=h: (T.wk[rows(a), 8 + 4 * h:9 + 4 * h], T.kap[rows(h), :]), [v("wk", 8 + 4 * h, 12 + 4 * h)], [], 5000)
     for h in range(2):
-        dma("Y", "lq%d" % h, lambda a, h=h: (T["Q%d" % h][rows(a), H:], T.pa[rows(h), :]), [Qs[h]], [], 9000 + 4000 * h)
+        dma("Y", "lq%d" % h, lambda a, h=h: (T["Q%d" % h][rows(a), 0:W], T.pa[rows(h), :]), [Qs[h]],
+            [Xs[0], Qs[0]][:1 + h] if PAR["dq"] else [], 6000 - 1500 * h if PAR["dq"] else 9000 + 4000 * h)
 
     iota(v("D0"), [[1, 128]], 0, -1)
     iota(v("pI", 0, 1), [[0, 1]], 0, 1)
-    iota(v("sm", 0, 24), [[0, 3], [1, 8]], 0, 0)
+    iota(v("sm", 0, 32), [[0, 4], [1, 8]], 0, 0)
     iota(v("KK"), [[0, 8], [1, 16]], 0, 0)
-    iota(v("sm", 32, 48), [[2, 2], [0, 8]], 12, 16)
-    iota(v("sm", 48, 56), [[0, 8]], 13, 16)
+    iota(v("sm", 32, 40), [[0, 8]], 13, 16)
+    iota(v("sm", 40, 56), [[2, 2], [0, 8]], 12, 16)
+    iota(v("sm", 56, 64), [[0, 8]], W + 14, 0)
     iota(v("C144"), [[1, 144]], -15, 0)
-    iota(v("q18"), [[1, 8], [0, 18]], 0, 0)
-    iota(v("t18"), [[0, 8], [1, 18]], 0, 0)
-    iota(v("G16"), [[16, 8], [0, 16]], 0, 0)
-    iota(v("sm", 64, 80), [[1, 16]], 0, 0)
-    iota(v("col", 16, 17), [[0, 1]], -H, 1)
-    iota(v("NUM"), [[1, W + H]], -H, 0)
-    for j in range(MD):
-        ts(v("II", 128 * j, 128 * j + 128), v("D0"), 0.0, eq)
-    Ib, nI = v("II", 0, 128), v("nI")
-    act(nI, Ib, ACT.Copy, scale=-1.0); act(v("I2"), Ib, ACT.Copy, scale=2.0)
-    ts(v("pI", 1, 2), v("pI", 0, 1), 15, band)
-    ts(v("pI", 2, 3), v("pI", 0, 1), 4, ALU.arith_shift_right)
-    ts(v("pI", 3, 4), v("pI", 0, 1), 7, band)
-    ts(v("pI", 4, 5), v("pI", 1, 2), 3, ALU.arith_shift_right)
-    ts(v("pI", 5, 6), v("pI", 0, 1), 6, ALU.arith_shift_right)
+    iota(v("sm", 64, 73), [[16, 9]], 0, 0)
+    iota(v("sm", 80, 88), [[2, 8]], 2, 0)
+    iota(v("t18"), [[0, 8], [1, 18]], -2, 0)
+    Ib, nI, db, BLK = v("Ib"), v("nI"), v("db"), v("BLK")
+    ts(Ib, v("D0"), 0.0, eq)
+    act(nI, Ib, ACT.Copy, scale=-1.0); act(v("I32"), Ib, ACT.Copy, scale=1.0 / 32); act(v("I2"), Ib, ACT.Copy, scale=2.0)
+    for j, (s, o) in enumerate(((15, band), (4, shr), (7, band), (6, shr))):
+        ts(v("pI", j + 1, j + 2), v("pI", 0, 1), s, o)
+    ts(v("pI", 5, 6), v("pI", 0, 1), 15, band, 3, shr)
     cp(v("col", 0, 6), v("pI", 0, 6))
-    pr, pq, p7, p3, p64 = (v("col", j, j + 1) for j in (1, 2, 3, 4, 5))
+    pr, pq, p7, p64, p3 = (v("col", j, j + 1) for j in (1, 2, 3, 4, 5))
     p16, pr1, yb, pc, pr8, pr8k = (v("col", j, j + 1) for j in (6, 7, 8, 9, 10, 11))
     act(p16, pq, ACT.Copy, scale=16.0); act(pr1, pr, ACT.Identity, bias=1.0); act(pr8, pr, ACT.Copy, scale=8.0)
     act(pr8k, p64, ACT.Identity, scale=float(K), bias=pr8)
@@ -213,199 +251,261 @@ def build(T, send):
     cp(v("col", 12, 14), v("wk", 0, 8, 4)); cp(v("col", 14, 16), v("wk", 8, 16, 4))
     wc, kc = [v("col", 12 + h, 13 + h) for h in range(2)], [v("col", 14 + h, 15 + h) for h in range(2)]
     q8 = v("sm", 0, 8)
-    b16, bm16, b32, bm32, b64, bm64 = (v("b8", 8 * j, 8 * j + 8) for j in range(6))
+    b16, bm32 = v("b8", 0, 8), v("b8", 8, 16)
     ts(b16, q8, pq, eq, 16.0, mul)
-    for b, c in ((bm16, -1.0), (b32, 2.0), (bm32, -2.0), (b64, 4.0), (bm64, -4.0)):
-        act(b, b16, ACT.Copy, scale=c)
-    ms(v("c1"), 1.0); ms(v("c1", 0, 104, 13), -1.0e6); ms(v("c2"), -1.0); ms(v("c2", 0, 144, 18), 2.0e7)
-    ms(v("p4", 305, 432, 18), 1.0e7); ms(v("p5", 305, 432, 18), 1.0e7)
-    bc16, bcq, perm = v("lists", 0, 8), v("lists", 8, 17), v("lists", 18, 26)
+    act(bm32, b16, ACT.Copy, scale=-2.0)
+    if PAR["ut"]:
+        act(v("q8e"), b16, ACT.Copy, scale=1.0 / 16)
+    ms(v("c1"), 1.0); ms(v("c1", 0, 104, 13), -1.0e6); ms(v("c2"), 1.0); ms(v("c2", 0, 136, 17), -1.0e6)
+    ms(v("zc"), 1.0); ms(v("zc", 0, 144, 18), 0.0); ms(v("zc", 1, 144, 18), 0.0); ms(v("zc", 144, 160, 2), 0.0)
+    ms(v("Acol", 0, 1), -0.484375); ms(v("x", 0, 16), 0.0)
+    bc16, bcq, perm = v("lists", 0, 8), v("lists", 8, 17), v("lists", 18, 27)
     cp(bc16, q8)
-    act(v("eqtab"), v("KK"), ACT.Identity, scale=-1.0, bias=12.0)
-    ts(v("db"), v("KK"), pr, eq)
-    ts(v("L1", 0, 24), v("sm", 0, 24), pq, eq, -1.0, mul)
-    ts(v("sm", 96, 120), v("sm", 0, 24), pq, eq)
-    tt(v("L1", 24, 48), v("sm", 96, 120), v("sm", 32, 56), mul)
+    ts(db, v("KK"), pr, eq)
+    ts(v("L1", 0, 32), v("sm", 0, 32), pq, eq, -1.0, mul)
+    ts(v("sm", 96, 128), v("sm", 0, 32), pq, eq)
+    tt(v("L1", 32, 64), v("sm", 96, 128), v("sm", 32, 64), mul)
     ts(v("Sel"), v("C144"), p16, eq)
-    act(v("LBb"), v("Sel"), ACT.Copy, scale=pr1); act(v("LBf"), v("Sel"), ACT.Copy, scale=pr1)
-    act(v("tm", 0, 9), v("sm", 64, 73), ACT.Identity, scale=16.0, bias=pr)
+    act(v("tm", 0, 9), v("sm", 64, 73), ACT.Identity, bias=pr)
     ts(v("smi", 0, 9), v("tm", 0, 9), 1.0 / 18, mul, 0.5 / 18 - 0.5, addo); cp(bcq, v("smi", 0, 9))
-    act(v("tm", 16, 24), q8, ACT.Identity, scale=2.0, bias=pc); ts(perm, v("tm", 16, 24), 1.0, addo)
-    BLK = v("BLK")
-    ts(BLK, v("G16"), p16, eq)
-    for h in range(2):
-        part = lambda name: v(name, 144 * h, 144 * h + 144)
-        act(part("Wsel"), v("Sel"), ACT.Copy, scale=wc[h])
-        ts(part("kd"), v("t18"), pr1, eq, kc[h], mul)
-        mm([(v("p%d" % (6 + h), 0, 144), [(BLK, part("kd"))])])
-        act(part("KapT"), v("p%d" % (6 + h), 0, 144), ACT.Copy)
-    ms(v("Acol", 0, 1), -0.484375)
-    act(v("NC", 0, 8), q8, ACT.Identity, scale=128.0, bias=pr8k); act(v("NC", 8, 16), q8, ACT.Identity, scale=128.0, bias=pr8)
-    le2, eq1, le0, gtk, kb = (v("tb", 128 * j, 128 * j + 128) for j in range(5))
-    F1, FE, FA, FB, FC, FD = (v("F", 128 * j, 128 * j + 128) for j in range(6))
-    tt(kb, v("KK"), BLK, mul)
-    keep(le2, BLK, ALU.is_ge, 2, -1); keep(eq1, BLK, eq, -1, 1); keep(le0, BLK, ALU.is_ge, 0, -1); keep(gtk, kb, ALU.is_ge, -3, 1)
-    for o, i, c in ((F1, le2, -4096.0), (FE, eq1, 32.0), (FA, gtk, -32.0), (FB, gtk, -5.0), (FC, le0, 32768.0), (FD, eq1, -16384.0)):
-        act(o, i, ACT.Copy, scale=c)
-    ts(v("Z1", 0, 144), v("q18"), pq, eq, 8192.0, mul)
-    act(v("t18"), v("t18"), ACT.Identity, scale=-1.0, bias=-14.5)
-    tt(v("Z2", 0, 144), v("Z1", 0, 144), v("t18"), mul)
-    act(v("Z1", 144, 288), v("Z1", 0, 144), ACT.Copy, scale=-1.0); act(v("Z2", 144, 288), v("Z2", 0, 144), ACT.Copy, scale=-1.0)
-    ms(v("Z1", 0, 144, 18), 0.0); ts(v("Z2", 0, 144, 18), q8, pq, eq, v("col", 16, 17), mul)
+    ts(v("lists", 18, 26), v("sm", 80, 88), pc, addo); ts(v("lists", 26, 27), p7, 2.0, mul, 145.0, addo)
     ms(v("ones"), 1.0)
+    iota(v("G16"), [[16, 8], [0, 16]], 0, 0); ts(BLK, v("G16"), p16, eq)
+    ts(v("e18", 0, 144), v("t18"), pr, eq); ts(v("e18", 144, 288), v("t18"), pr1, eq)
+    tt(v("e18", 288, 432), v("e18", 0, 144), v("e18", 144, 288), sub)
+    for h in range(2):
+        ts(xv(h, W, W + 16), v("KK", 0, 16), -2.0, addo, pr, eq)
+        if PAR["ut"]:
+            act(hv("Wsel", h, 144, 0, 8), v("q8e"), ACT.Copy, scale=wc[h])
+        else:
+            act(hv("Wsel", h, 144), v("Sel"), ACT.Copy, scale=wc[h])
+        act(hv("kd", h, 144), v("e18", 288, 432), ACT.Copy, scale=kc[h])
+        mm([(v("p%d" % (6 + h), 0, 144), [(BLK, hv("kd", h, 144))])])
+        act(hv("KapT", h, 144), v("p%d" % (6 + h), 0, 144), ACT.Copy)
+        ts(hv("z1", h, 160, 144, 160, 2), q8, 128.0, mul, pr8k, addo)
+    tag[2] = "g"
+    FH, FW, Ff = v("FH"), v("FW"), v("Ff")
+    D = [[1, 128]]
+    iota(FH, [[0, 128]], 0, 0); keep(FH, FH, D, ge, -128.0, -3, -1); keep(FH, FH, D, ne, 4096.0, -1, -1); tt(FH, FH, BLK, mul)
+    iota(Ff, [[0, 8], [-37, 16]], 0, 0); keep(FW, Ff, D, ge, 0.0, -3, -1); keep(FW, FW, D, ge, 8192.0, -1, -1)
+    keep(FW, FW, D, ne, -8192.0, -1, -1); tt(FW, FW, BLK, mul)
+    Z1, Z2, Z3, q18, S18 = v("Z1"), v("Z2"), v("Z3"), v("q18"), [[0, 8], [1, 18]]
+    iota(q18, [[1, 8], [0, 18]], 0, 0); keep(Z1, q18, S18, ge, -1.0, -2, 0); ts(Z1, Z1, pq, eq, 8192.0, mul)
+    iota(Z2, [[0, 8], [8192, 18]], -8192 * 17 - 4096, 0); keep(Z2, Z2, S18, ne, -4194304.0, 0, 0); keep(Z2, Z2, S18, ne, float(W), -1, 0)
+    ts(q18, q18, pq, eq); tt(Z2, Z2, q18, mul)
+    ts(Z3, q8, pq, eq, v("col", 0, 1), mul)
+    n = PAR["num"]
+    iota(v("NUM", 0, n), [[1, n]], 0, 0); iota(v("NUM", W), [[0, H]], 0, 0)
+    for c in range(n, W, 512):
+        act(v("NUM", c, c + 512), v("NUM", 0, 512), ACT.Identity, bias=float(c))
+    act(v("LBb"), v("Sel"), ACT.Copy, scale=pr1)
+    tag[:] = [1, 0, "g"]
+    gcopy(v("LBf"), v("LBb"))["late"] = True
+    keep(v("LBa", 0, 144), v("LBb"), [[0, 144]], ge, 0.0, 63, -1)["late"] = True
+    keep(v("LBa", 144, 288), v("LBb"), [[0, 144]], ge, 0.0, -64, 1)["late"] = True
+    tag[:] = [0, 0, "c"]
     cp(v("R0", 0, H), v("rp32", 0, H)); cp(v("R0", H, P), v("rp32", H, P))
 
-    def sel(name, r, lo=0):
-        return v(name, lo + 15 - r, lo + 143 - r)
+    def sel(name, r, lo=0, a=None):
+        return v(name, lo + 15 - r, lo + 143 - r, 1, a)
 
+    fcp = gather if PAR["fx"] else cp
     big = [0, 0]
 
     def bank(h):
         big[h] += 1
         return "p%d" % (2 * h + big[h] % 2)
 
-    def hv(name, h, n=H, lo=0, hi=None, st=1):
-        return v(name, h * n + lo, h * n + (n if hi is None else hi), st)
+    X1, MK = (5, 6) if PAR["n3"] else (2, 3)
 
-    def near(h):
-        return [v("X%d" % h, c, c + H) for c in (0, 2 * H, H)]
+    def near(h, j, n=1):
+        return v("X%d" % h, W + j * H, W + (j + n) * H)
 
     def jumps(vis, h):
-        tag[1] = h
+        tag[:] = [vis, h, "x"]
         R, pv, ps, X = "R%d" % vis, "p%d" % (4 + h), "p%d" % (6 + h), Xs[h]
-        xk = lambda k: hv("x", h, 2048, k, None, 16)
-        for j in range(4):
-            gather(hv("x", h, 2048, 512 * j, 512 * j + 512), ind(X, hv(R, h, H, 32 * j, 32 * j + 32)))
-        for jj, ks in enumerate(([1, 2, 3, 4], [5, 6, 7], [8, 9, 10], [11, 12, 13])):
-            b = bank(h); k0 = ks[0]
-            mm([(v(b, H * j, H * j + H), [(Ib, xk(k + 1)), (nI, xk(k))]) for j, k in enumerate(ks)])
-            o, i = hv("ab", h, 13 * H, H * (k0 - 1), H * (k0 - 1 + len(ks))), v(b, 0, H * len(ks))
-            ak = lambda k: hv("ab", h, 13 * H, H * (k - 1), H * k)
-            if PAR["d"][2 * vis + h][jj] == "S":
-                act(o, i, ACT.Abs)
+        n = PAR["nx"]
+        for j in range(n):
+            gather(xv(h, W // n * j, W // n * (j + 1)), ind(X, hv(R, h, H, H // n * j, H // n * (j + 1))))
+        tag[2] = "j"
+        if PAR["jb"] == 3:
+            for j in range(4):
+                b = v(bank(h), 0, 512)
+                mm([(b, [(Ib, xv(h, 512 * j, 512 * j + 512)), (nI, xv(h, 512 * j - 1, 512 * j + 511))])])
+                act(hv("ab", h, 13 * H, 416 * j, 416 * j + 416), b + ((2, 15),), ACT.Abs)
+            mm([(v(pv, k, 104, 13), [(hv("ab", h, 13 * H, k, None, 13), b16)]) for k in range(13)])
+        elif PAR["jb"] == 1:
+            xk = lambda k: xv(h, k, W, 16)
+            for ks in (range(1, 5), range(5, 8), range(8, 11), range(11, 14)):
+                ak = lambda k, n=1: hv("ab", h, 13 * H, H * (k - 1), H * (k - 1 + n))
+                b = bank(h)
+                mm([(v(b, H * j, H * j + H), [(Ib, xk(k + 1)), (nI, xk(k))]) for j, k in enumerate(ks)])
+                act(ak(ks[0], len(ks)), v(b, 0, H * len(ks)), ACT.Abs)
                 mm([(v(pv, k - 1, 104, 13), [(ak(k), b16)]) for k in ks])
-            else:
-                ts(o, i, 0.0, mxo)
-                mm([(v(pv, k - 1, 104, 13), [(ak(k), b32), (xk(k + 1), bm16), (xk(k), b16)]) for k in ks])
+        else:
+            for a, ks in ((a, ks) for a in range(2) for ks in (range(1, 8), range(8, 14))):
+                xk = lambda k: xv(h, K * a + k, K * a + K, 16)
+                ak = lambda k, n=1: hv("ab", h, 13 * H, 64 * (13 * a + k - 1), 64 * (13 * a + k - 1 + n))
+                b = bank(h)
+                mm([(v(b, 64 * j, 64 * j + 64), [(Ib, xk(k + 1)), (nI, xk(k))]) for j, k in enumerate(ks)])
+                act(ak(ks[0], len(ks)), v(b, 0, 64 * len(ks)), ACT.Abs)
+                mm([(v(pv, k - 1, 104, 13, a), [(ak(k), b16)]) for k in ks])
+        tag[2] = "a"
         scan(hv("s1", h, 104), v("c1"), v(pv, 0, 104), addo, mxo)
         ts(hv("ri", h, 8), hv("s1", h, 104, 12, None, 13), 15, band)
-        tt(hv("rT", h), ind(hv("ri", h, 8), bc16), v("db"), mul)
-        tt(hv("eqT", h), ind(hv("ri", h, 8), bc16), v("eqtab"), eq)
-        mm([(v(pv, 104, 128), [(hv("rT", h), v("L1", 0, 24)), (v("db"), v("L1", 24, 48))])])
-        mm([(v(ps, 0, MD * H), [(hv("eqT", h), v("II"))])])
-        cp(hv("pl", h, 24), v(pv, 104, 128))
-        gather(v(X[0], 0, XF), ind(hv("x", h, 2048), hv("pl", h, 24)))
-        act(hv("mask", h, MD * H), v(ps, 0, MD * H), ACT.Copy)
-        xp = near(h)[1]
-        mm([(v(pv, 128, 136), [(sel("Wsel", r, 144 * h), v(X[0], xp[1] + r, xp[2], 16)) for r in range(16)])])
-        cp(hv("ur", h, 8), v(pv, 128, 136))
-        ts(hv("u", h, 8), hv("ur", h, 8), W - 1, band)
-        tt(hv("uu", h, 8), hv("u", h, 8), hv("u", h, 8), mul)
-        tt(hv("z1", h, 144), ind(hv("u", h, 8), bcq), hv("KapT", h, 144), mul)
-        ts(hv("ua", h, 8), hv("uu", h, 8), 1.0 / 32, mul, v("Acol", vis, vis + 1), addo)
-        tt(hv("z2", h, 144), ind(hv("ua", h, 8), bcq), hv("z1", h, 144), addo)
-        ts(hv("CL", h, 144), hv("z2", h, 144), W - 1, band)
-        cp(hv("cl", h), ind(hv("CL", h, 144), perm))
-        m1 = hv("mask", h, MD * H, 0, H)
-        cp(hv("R16", h), hv(R, h))
-        ts(v("Q%d" % h, 0, H), hv(R, h), 262144.0, addo)
-        mm([(v(ps, 0, H), [(Ib, hv("R16", h)), (F1, m1)]),
-            (v(ps, 256, 384), [(nI, hv("R16", h)), (FA, m1), (FB, m1), (FC, m1), (FD, m1)])])
-        mm([(v(pv, 0, H), [(FE, m1)])])
-        act(hv("H0", h), v(ps, 0, H), ACT.Relu)
-        act(v(ps, 384, 512), v(ps, 256, 384), ACT.Relu, bias=4096.0)
-        tt(hv("Hh", h), hv("H0", h), v(pv, 0, H), addo)
-        ts(hv("u7", h, 8), hv("u", h, 8), 7, band)
-        tt(hv("n32", h, 8), hv("u7", h, 8), hv("NC", int(vis == TV - 1), 8), addo)
-        cp(hv("nl", h, 8), hv("n32", h, 8))
+        tt(hv("rT", h), ind(hv("ri", h, 8), bc16), db, mul)
+        mm([(v(pv, 104, 136), [(db, v("L1", 32, 64)), (hv("rT", h), v("L1", 0, 32))])])
+        (gather if PAR["su"] else cp)(hv("pl", h, 32), v(pv, 104, 136))
+        gather(near(h, 0), ind(xv(h, 0, W + 16), hv("pl", h, 32, 0, 8)))
+        if X1 == 2:
+            gather(near(h, 1, 3), ind(xv(h, 0, W + 16), hv("pl", h, 32, 8, 32)))
+        else:
+            gather(near(h, X1, 2), ind(xv(h, 0, W + 16), hv("pl", h, 32, 16, 32)))
+            gather(near(h, 1), ind(xv(h, 0, W + 16), hv("pl", h, 32, 8, 16)))
+        for n in (1, 2):
+            if n < MD:
+                fcp(near(h, MK + n, n), near(h, MK, n))
+        if "V" in PAR["b"][2 * vis + h]:
+            for n in (1, 2):
+                cp(near(h, X1 + 1 - 2 * n, n), near(h, X1 + 1 - n, n))
+        u = hv("u", h, 8)
+        if PAR["ut"]:
+            mm([(v(pv, 136, 144), [(near(h, 0), hv("Wsel", h, 144, 0, 8))])])
+            cp(hv("ur", h, 8), v(pv, 136, 144))
+            ts(hv("ut", h, 8), hv("ur", h, 8), W - 1, band)
+            tt(hv("uT", h), ind(hv("ut", h, 8), bc16), db, mul)
+            mm([(v(pv, 408, 416), [(hv("uT", h), v("q8e"))])])
+            cp(u, v(pv, 408, 416))
+        else:
+            mm([(v(pv, 136, 144), [(sel("Wsel", r, 144 * h), v(X[0], W + r, W + H, 16)) for r in range(16)])])
+            fcp(hv("ur", h, 8), v(pv, 136, 144))
+            ts(u, hv("ur", h, 8), W - 1, band)
+        tt(hv("z1", h, 160, 0, 144), ind(u, bcq), hv("KapT", h, 144), mul)
+        a = tt(hv("uu", h, 8), u, u, mul)
+        if PAR["fx"]:
+            ops.pop(); b = act(hv("uu", h, 8), u, ACT.Square); b["opt"] = {"S": (b["fns"], b["cost"]), "V": (a["fns"], a["cost"])}
+        ts(hv("z1", h, 160, 145, 160, 2), u, 7, band)
+        if PAR["fx"]:
+            affine(hv("z1", h, 160, 1, 144, 18), hv("uu", h, 8), 1.0 / 32, v("Acol", vis, vis + 1))
+        else:
+            ts(hv("z1", h, 160, 1, 144, 18), hv("uu", h, 8), 1.0 / 32, mul, v("Acol", vis, vis + 1), addo)
+        scan(hv("z2", h, 160), v("zc"), hv("z1", h, 160), mul, addo)
+        ts(hv("CL", h, 160), hv("z2", h, 160), W - 1, band)
+        cp(hv("cl", h, 144), ind(hv("CL", h, 160), perm))
+        tag[2] = "p"
+        (gather if PAR["t4"] else cp)(hv("R16", h), hv(R, h))
+        affine(v("Q%d" % h, W), hv("R16", h), 1.0, 8192.0)
+        mm([(v(ps, 0, H), [(v("I32"), hv("R16", h)), (FH, near(h, MK))]), (v(ps, H, 2 * H), [(nI, hv("R16", h)), (FW, near(h, MK))])])
+        ts(hv("Hh", h), v(ps, 0, H), 0.0, mxo, 2049.0, mn)
+        ts(v(ps, H, 2 * H), v(ps, H, 2 * H), -4096.484375, mxo, -2047.515625, addo)
+        mm([(v(ps, 256, 400), [(db, Z2), (db, Z3, v(ps, 257, 400, 18))])], last=False)
 
     def sums(h):
-        tag[1] = h
-        for j in range(2):
-            part = lambda name: hv(name, h, K, 512 * j, 512 * j + 512)
-            cp(part("Q16"), part("Qk"))
-            b = bank(h)
-            mm([(v(b), [(sel("LBb", 0), part("Q16")), (sel("LBb", 1), part("Xk"))])])
-            act(part("Y"), v(b), ACT.Copy)
+        tag[:] = [TV - 1, h, "y"]
+        for a in range(2):
+            gcopy(hv("Q16", h, K, a=a), v("Q%d" % h, K * a, K * a + K, 1, a))["late"] = True
+        b = bank(h)
+        mm([(v(b, 0, H), [(sel("LBa", 2 * j + 1, 144 * a), v("X%d" % h, K * a + H * j, K * a + H * j + H)) for j in range(8) for a in range(2)]
+             + [(sel("LBb", 2 * j), hv("Q16", h, K, H * j, H * j + H)) for j in range(8)])])
+        gather(hv("Yc", h), v(b, 0, H))
+        dma("Y", "yc%d" % h, lambda i: (T.Y[64 * (i // 2) + i % 2:64 * (i // 2) + 64:16, W * h + K * (i // 2):W * h + K * (i // 2) + K],
+                                        T.Yc[64 * (i // 2) + i % 2:64 * (i // 2) + 64:2, H * h:H * h + H]), [hv("Y", h, W)], [hv("Yc", h)], 2400, 4)
 
     def stores(vis, h):
-        tag[1] = h
-        for name, tab, lo, src, lat in (("x", Xs[h], XF, "m2", 2400), ("q", Qs[h], H, "S2", 3000)):
-            cp(ind(tab, hv("nl", h, 8)), hv(src, h))
-            dma("Y", "e%s%d%d" % (name, vis, h), lambda a, t=tab[0], lo=lo: (T[t][rows(1 - a), lo + K * a:lo + K * a + K], T[t][rows(a), lo + K * a:lo + K * a + K]),
-                [tab], [tab], lat)
-            if vis == TV - 2:
-                k = name.upper() + "k"
-                dma("Y", "k%s%d" % (name, h), lambda a, t=tab[0], lo=lo, k=k: (T[k][rows(a), K * h:K * h + K], T[t][rows(a), lo + K * a:lo + K * a + K]),
-                    [hv(k, h, K)], [tab], lat)
+        tag[:] = [vis, h, "s"]
+        for name, tab, src, lat in (("x", Xs[h], "m2", 2400), ("q", Qs[h], "S2", 3000)):
+            cp(ind(tab, hv("cl", h, 144, H, H + 8)), hv(src, h))
+            dma("Y", "e%s%d%d" % (name, vis, h), lambda a, t=tab[0]: (T[t][rows(1 - a), K * a:K * a + K], T[t][rows(a), K * a:K * a + K]),
+                [tab], [tab, Xs[h]] if PAR["de"] else [tab], lat)
 
     def rivals(vis, h):
-        tag[1] = h
+        tag[:] = [vis, h, "r"]
         pv, X, Q = "p%d" % (4 + h), Xs[h], Qs[h]
-        for j in range(4):
-            gather(hv("Xc", h, 2048, 512 * j, 512 * j + 512), ind(X, hv("cl", h, H, 32 * j, 32 * j + 32)), 2.0)
-        for j in range(2):
-            for m in range(8 * j, 8 * j + 8, MD):
-                tt(hv("am", h, 2048, H * m, H * (m + MD)), ind(Q, hv("cl", h, H, 8 * m, 8 * (m + MD))), hv("mask", h, MD * H), mul)
-            mm([(v(pv, 136 + 64 * j, 200 + 64 * j), [(sel("Sel", r), hv("am", h, 2048, 1024 * j + r, 1024 * j + 1024, 16)) for r in range(16)])])
-            cp(hv("bl", h, H, 64 * j, 64 * j + 64), v(pv, 136 + 64 * j, 200 + 64 * j))
-            for i in range(2):
-                c = 64 * j + 32 * i
-                gather(hv("Xb", h, 2048, 16 * c, 16 * c + 512), ind(X, hv("bl", h, H, c, c + 32)))
+        n = PAR["nc"]
+        for j in range(n):
+            gather(hv("Xc", h, W, W // n * j, W // n * (j + 1)), ind(X, hv("cl", h, 144, H // n * j, H // n * (j + 1))), 2.0)
+        n = PAR["ns"]; c = H // n
+        for j in range(n):
+            for m in range(16 // n * j, 16 // n * (j + 1), MD):
+                tt(hv("am", h, W, H * m, H * (m + MD)), ind(Q, hv("cl", h, 144, 8 * m, 8 * (m + MD))), near(h, MK, MD), mul)
+            mm([(v(pv, 144 + c * j, 144 + c * j + c), [(sel("Sel", r), hv("am", h, W, 16 * c * j + r, 16 * c * (j + 1), 16)) for r in range(16)])])
+            (gather if PAR["su"] else cp)(hv("bl", h, H, c * j, c * j + c), v(pv, 144 + c * j, 144 + c * j + c))
+            for i in range(4 // n * j, 4 // n * (j + 1)):
+                o, w = hv("Xb", h, W, 512 * i, 512 * i + 512), ind(X, hv("bl", h, H, 32 * i, 32 * i + 32))
+                if PAR["b"][2 * vis + h][i] == "V":
+                    tt(o, w, near(h, X1 - 3, 4), addo)
+                else:
+                    gather(o, w)
 
     def scores(vis, h):
-        tag[1] = h
+        tag[:] = [vis, h, "e"]
         pv = "p%d" % (4 + h)
-        xm, xp, x1 = near(h)
-        blocks = [[(0, v("I2"), xp, bm64, xm)]]
+        ot = lambda t, n=1: hv("mx", h, 17 * H, H * t, H * (t + n))
+        b = bank(h)
+        mm([(v(b, 0, H), [(v("I2"), near(h, 0)), (nI, near(h, 1)), (nI, near(h, X1))])])
+        act(ot(0), v(b, 0, H), ACT.Abs)
+        mm([(v(pv, 272, 408, 17), [(ot(0), bm32)])])
         for j in range(4):
-            blocks.append([(m + 1, Ib, hv("Xc", h, 2048, H * m, H * m + H), bm32, hv("Xb", h, 2048, H * m, H * m + H)) for m in range(4 * j, 4 * j + 4)])
-        for j, bl in enumerate(blocks):
-            b = bank(h); n = H * len(bl); t0 = bl[0][0]
-            o = hv("mx", h, 17 * H, H * t0, H * t0 + n); ot = lambda t: hv("mx", h, 17 * H, H * t, H * t + H)
-            if PAR["e"][2 * vis + h][j] == "V":
-                mm([(v(b, H * i, H * i + H), [(l, c), (nI, x1)]) for i, (t, l, c, s, xb) in enumerate(bl)])
-                tt(o, v(b, 0, n), v(bl[0][4][0], bl[0][4][1], bl[0][4][1] + n), mxo)
-                mm([(v(pv, 288 + t, 432, 18), [(ot(t), b64), (c, s), (xb, bm32)]) for (t, l, c, s, xb) in bl])
+            b = v(bank(h), 0, 512); c, xb = (hv(a, h, W, 512 * j, 512 * j + 512) for a in ("Xc", "Xb"))
+            if PAR["b"][2 * vis + h][j] == "V":
+                mm([(b, [(Ib, c)])], last=False)
+            elif "V" in PAR["b"][2 * vis + h]:
+                mm([(b, [(Ib, c), (nI, near(h, X1 - 3, 4))])], last=False)
             else:
-                mm([(v(b, H * i, H * i + H), [(l, c), (nI, x1), (nI, xb)]) for i, (t, l, c, s, xb) in enumerate(bl)])
-                act(o, v(b, 0, n), ACT.Abs)
-                mm([(v(pv, 288 + t, 432, 18), [(ot(t), b32), (x1, bm32)]) for (t, l, c, s, xb) in bl])
+                mm([(b, [(Ib, c)] + [(nI, near(h, X1), v(b[0], H * i, H * i + H)) for i in range(4)])], last=False)
+            mm([(b, [(nI, xb)])], first=False)
+            act(ot(4 * j + 1, 4), b, ACT.Abs)
+            mm([(v(pv, 272 + t, 408, 17), [(ot(t), bm32)]) for t in range(4 * j + 1, 4 * j + 5)])
 
     def splice(vis, h):
-        tag[1] = h
-        pv = "p%d" % (4 + h)
-        scan(hv("s2", h, 144), v("c2"), v(pv, 288, 432), addo, mn)
-        ts(hv("twi", h, 8), hv("s2", h, 144, 17, None, 18), 31, band)
-        tt(hv("tT", h), ind(hv("twi", h, 8), bc16), v("db"), mul)
-        mm([(v(pv, 0, 288), [(hv("tT", h), v("Z1")), (v("db"), v("Z2"))])])
-        tt(hv("sb", h, 144), hv("CL", h, 144), v(pv, 0, 144), mn)
-        scan(hv("cwf", h, 144), v(pv, 144, 288), hv("sb", h, 144), mn, mxo)
-        won = hv("cwf", h, 144, 17, None, 18); cw = hv("cw", h, 8)
-        ts(cw, won, float(H), addo)
+        tag[:] = [vis, h, "w"]
+        pv, ps = "p%d" % (4 + h), "p%d" % (6 + h)
+        scan(hv("s2", h, 136), v("c2"), v(pv, 272, 408), addo, mxo)
+        ts(hv("twi", h, 8), hv("s2", h, 136, 16, None, 17), 31, band)
+        tt(hv("tT", h), ind(hv("twi", h, 8), bc16), db, mul)
+        mm([(v(ps, 256, 400), [(hv("tT", h), Z1)])], first=False)
+        scan(hv("cwf", h, 144), v(ps, 256, 400), hv("CL", h, 160, 0, 144), addo, mxo)
+        cw = hv("cw", h, 8)
+        ts(hv("cwi", h, 8), hv("cwf", h, 144, 17, None, 18), 2 * W - 1, band)
+        fcp(cw, hv("cwi", h, 8))
         tt(hv("t1", h), ind(v("NUM"), cw), hv("Hh", h), mul)
-        ts(hv("t2", h), hv("t1", h), 1.0 / 32, mul, 8192 - 0.484375, addo)
-        tt(hv("t3", h), hv("t2", h), v("p%d" % (6 + h), 384, 512), sub)
-        tt(hv("t4", h), ind(v("Q%d" % h), cw), hv("t3", h), mxo)
+        if PAR["t4"]:
+            gather(hv("Qw", h), ind(v("Q%d" % h), cw))
+            tt(v(ps, H, 2 * H), hv("t1", h), v(ps, H, 2 * H), sub)
+            tt(hv("t4", h), hv("Qw", h), v(ps, H, 2 * H), mxo)
+        else:
+            tt(hv("t3", h), hv("t1", h), v(ps, H, 2 * H), sub)
+            tt(hv("t4", h), ind(v("Q%d" % h), cw), hv("t3", h), mxo)
         ts(hv("S2", h), hv("t4", h), W - 1, band)
         last = vis == TV - 1
         src, dst = ("Of", "Rf") if last else ("O%d" % vis, "R%d" % (vis + 1))
-        cp(hv(src, h), hv("S2", h))
-        s = add("G", [lambda q: send(q, ap(hv(dst, h)), ap(hv(src, h)), "ar%d%d" % (vis, h), last)], [], [hv(src, h)], 500.0, remote=True)
+        fcp(hv(src, h), hv("S2", h))
+        s = add("G", [lambda q: send(q, ap(hv(dst, h)), ap(hv(src, h)), "ar%d%d" % (vis, h), last)], [], [hv(src, h)],
+                COST["SEND"] + COST["FIRST"] * (vis + h == 0), remote=True)
         add("N", [], [hv(dst, h)], [], 0.0, sem="ar%d%d" % (vis, h), lat=COST["LINK"], after=s, last=last)
-        tt(hv("m1", h), ind(v("X%d" % h, XF - H), cw), near(h)[2], addo)
-        if not last:
-            ts(hv("m2", h), hv("m1", h), 0.5, mul, -0.25, addo)
-            act(hv("sg", h, 8), won, ACT.Sign, bias=0.5)
+        if PAR["m1"] == "V":
+            m1 = hv("m1", h)
+            tt(m1, ind(v("X%d" % h, 0, W + H), cw), near(h, X1), addo)
         else:
-            ts(hv("m16", h), hv("m1", h), 0.5, mul, 1023.75, addo)
-            b = bank(h); Y = hv("Y", h, K)
-            mm([(v(b, 0, H), [(sel("LBf", 0), hv("Of", h)), (sel("LBb", 1), hv("m16", h))])])
+            m1 = v(bank(h), 0, H)
+            gather(hv("m1", h), ind(v("X%d" % h, 0, W + H), cw))
+            mm([(m1, [(Ib, near(h, X1)), (Ib, hv("m1", h))])])
+        if not last:
+            affine(hv("m2", h), m1, 0.5, -0.25)
+            if PAR["t4"]:
+                act(hv("sg", h, 8), hv("cwi", h, 8), ACT.Sign, scale=-1.0, bias=W - 0.5)
+            else:
+                ts(hv("sg", h, 8), hv("cwi", h, 8), float(W), ALU.is_lt)
+        else:
+            affine(hv("m16", h), m1, 0.5, 1023.75)
+            b = bank(h); Y = hv("Y", h, W)
+            mm([(v(b, 0, H), [(sel("LBb", 1), hv("m16", h)), (sel("LBf", 0), hv("Of", h))])])
             act(hv("ys", h), v(b, 0, H), ACT.Identity, bias=yb)
-            cp(ind(Y, hv("nl", h, 8)), hv("ys", h))
-            dma("Y", "oq%d" % h, lambda a: (T.yq[4 * h:4 * h + 4, K * a:K * a + K], T.Y[64 * a:64 * a + 64:16, K * h:K * h + K]), [], [Y], 2000)
-            dma("YS"[h], "ox%d" % h, lambda a: (T.yx[4 * h:4 * h + 4, K * a:K * a + K], T.Y[64 * a + 1:64 * a + 64:16, K * h:K * h + K]), [], [Y], 2000)
-            dma("Y", "or%d" % h, lambda a: (T.yr[rows(h), H * a:H * a + H], T.Rf[rows(a), H * h:H * h + H]), [], [hv("Rf", h)], 2000)
+            cp(ind(Y, hv("cl", h, 144, H, H + 8)), hv("ys", h))
+            for j, (name, out) in enumerate((("oq", T.yq), ("ox", T.yx))):
+                dma("YS"[j * h], "%s%d" % (name, h), lambda a, j=j, out=out: (out[4 * h:4 * h + 4, K * a:K * a + K],
+                    T.Y[64 * a + j:64 * a + 64:16, W * h + K * a:W * h + K * a + K]), [], [Y], 2000)
+            dma("YS"[h * PAR["os"]], "or%d" % h, lambda a: (T.yr[rows(h), H * a:H * a + H], T.Rf[rows(a), H * h:H * h + H]), [], [hv("Rf", h)], 2000)
 
     for vis in range(TV):
         for h in range(2):
@@ -418,7 +518,10 @@ def build(T, send):
         if vis < TV - 1:
             b = bank(1)
             mm([(v(b, 0, 16), [(v("ones"), v("sg"))])])
-            act(v("aj"), v(b, 0, 16), ACT.Identity, bias=64 - 0.484375 / 16, scale=0.5, acc=v("Acol", vis + 1, vis + 2))
+            if PAR["t4"]:
+                act(v("aj"), v(b, 0, 16), ACT.Identity, bias=64 - 0.484375 / 16, scale=0.5, acc=v("Acol", vis + 1, vis + 2))
+            else:
+                act(v("aj"), v(b, 0, 16), ACT.Identity, bias=-0.484375 / 16, acc=v("Acol", vis + 1, vis + 2))
     return ops
 
 
@@ -427,16 +530,20 @@ def depend(ops):
     for i, o in enumerate(ops):
         dep = set()
         for acc, wr in ((o["r"], False), (o["w"], True)):
-            for (name, lo, hi, st) in acc:
+            for (name, lo, hi, st, a, *_) in acc:
                 ps = SCRATCH[name][0] == "psum"
-                for (j, l2, h2, w2) in seen.get(name, []):
-                    if j != i and ((l2 < hi and lo < h2 and (wr or w2)) or (ps and ops[j]["eng"] != o["eng"])):
+                for (j, l2, h2, s2, w2, a2) in seen.get(name, []):
+                    meet = l2 < hi and lo < h2 and (wr or w2) and (a is None or a2 is None or a == a2) and (st != s2 or (lo - l2) % st == 0)
+                    if j != i and (meet or (ps and ops[j]["eng"] != o["eng"]) or (ps and ("opt" in o or "opt" in ops[j]))):
                         dep.add(j)
         for acc, wr in ((o["r"], False), (o["w"], True)):
-            for (name, lo, hi, st) in acc:
-                seen.setdefault(name, []).append((i, lo, hi, wr))
-        o["dep"] = dep; o["id"] = i
+            for (name, lo, hi, st, a, *_) in acc:
+                seen.setdefault(name, []).append((i, lo, hi, st, wr, a))
         o["sdep"] = dep | ({o["after"]["id"]} if "after" in o else set())
+        if o.get("late"):
+            o["sdep"] |= {j for j in range(i) if ops[j].get("remote") and ops[j]["vis"] < o["vis"]}
+        o["dep"] = {j for j in dep if ops[j]["eng"] != "P"} if o.get("goes_on") else dep
+        o["id"] = i
     anc = []
     for o in ops:
         a = 0
@@ -448,31 +555,47 @@ def depend(ops):
         anc.append(a)
 
 
-def order(ops):
-    HOP, SAME = COST["HOP"], COST["SAME"]
-    succ = [[] for _ in ops]
-    for o in ops:
-        for j in o["sdep"]:
-            succ[j].append(o["id"])
+def chains(ops, succ):
     prio = [0.0] * len(ops)
     for o in reversed(ops):
-        prio[o["id"]] = o["cost"] + o.get("lat", 0) + max([prio[j] + HOP for j in succ[o["id"]]], default=0.0)
-    prio = [p + PAR["lead"] * (1 - o["half"]) + 100.0 * PAR["bias"].get("%s.%d" % (o["w"] or o["r"])[0][:2], 0) for p, o in zip(prio, ops)]
-    free = {e: 0.0 for e in "VSPGYN"}
-    left = [len(o["sdep"]) for o in ops]; rdy = [0.0] * len(ops); fin = [0.0] * len(ops)
-    pool = [o["id"] for o in ops if not o["sdep"]]; seq = []
-    while pool:
-        best = min(pool, key=lambda i: (max(rdy[i], free[ops[i]["eng"]]), -prio[i]))
-        e = ops[best]["eng"]; t0 = max(rdy[best], free[e])
-        i = max((i for i in pool if ops[i]["eng"] == e and rdy[i] <= t0 + PAR["look"]), key=lambda i: prio[i])
-        o = ops[i]; t0 = max(rdy[i], free[e])
-        free[e] = t0 + o["cost"]; fin[i] = free[e] + o.get("lat", 0); o["t0"] = t0
-        pool.remove(i); seq.append(i)
+        prio[o["id"]] = o["cost"] + o.get("lat", 0) + max([prio[j] + COST["HOP"] for j in succ[o["id"]]], default=0.0)
+    return prio
+
+
+def walk(ops, key, succ):
+    left = [len(o["sdep"]) for o in ops]; st = [0.0] * len(ops); done = [0.0] * len(ops); eng = [None] * len(ops)
+    free = {e: 0.0 for e in "VSPGYN"}; pool = {e: {} for e in free}
+    opts = [o.get("opt", {o["eng"]: (None, o["cost"])}) for o in ops]
+
+    def offer(i):
+        for e in opts[i]:
+            pool[e][i] = max([done[j] + ops[j].get("lat", 0) + (COST["SAME"] if eng[j] == e else COST["HOP"]) for j in ops[i]["sdep"]], default=0.0)
+
+    for i in range(len(ops)):
+        if not left[i]:
+            offer(i)
+    for _ in ops:
+        best = None
+        for e, p in pool.items():
+            for i, r in p.items():
+                t = max(r, free[e])
+                if e == "V" and len(opts[i]) > 1 and free["S"] < t + PAR["vpen"]:
+                    t = max(t, free["S"]) + 1.0
+                if best is None or t < best[0]:
+                    best = (t, e)
+        t, e = best; p = pool[e]
+        can = [i for i in p if not (e == "V" and len(opts[i]) > 1 and free["S"] < t + PAR["vpen"] and len(p) > 1)] or list(p)
+        i = min((i for i in can if p[i] <= t + PAR["look"]), key=lambda i: (key[i], i), default=min(can, key=lambda i: p[i]))
+        if p[i] > t:
+            i = min((j for j in can if p[j] <= t and t + opts[j][e][1] <= p[i] + PAR["fill"]), key=lambda j: (key[j], j), default=i)
+        st[i] = max(p[i], free[e]); done[i] = free[e] = st[i] + opts[i][e][1]; eng[i] = e
+        for q in opts[i]:
+            del pool[q][i]
         for j in succ[i]:
-            rdy[j] = max(rdy[j], fin[i] + (SAME if ops[j]["eng"] == e else HOP)); left[j] -= 1
-            if left[j] == 0:
-                pool.append(j)
-    return seq, max(fin)
+            left[j] -= 1
+            if not left[j]:
+                offer(j)
+    return st, done, eng
 
 
 def place(ops, key, pred, succ, back):
@@ -508,11 +631,11 @@ def refine(ops):
     for o in ops:
         for j in pred[o["id"]]:
             succ[j].append(o["id"])
-    if PAR["key"] is None:
-        order(ops)
-    key = PAR["key"] or [o["t0"] for o in ops]; best = None
+    key = PAR["key"] or [-p - 100.0 * PAR["lead"].get("%s%d%d" % (o["ph"], o["vis"], o["half"]), 0) for p, o in zip(chains(ops, succ), ops)]
+    key = [o["id"] - 1e9 if "sem" in o and not o["sdep"] else k for k, o in zip(key, ops)]
+    best = None
     for n in range(PAR["rounds"]):
-        st, done, eng = place(ops, key, pred, succ, False)
+        st, done, eng = walk(ops, key, succ) if PAR["walk"] else place(ops, key, pred, succ, False)
         end = max(d + o.get("lat", 0) for d, o in zip(done, ops))
         if best is None or end < best[0]:
             best = (end, st, eng)
@@ -523,6 +646,110 @@ def refine(ops):
         if "opt" in o:
             o["eng"] = e; o["fns"], o["cost"] = o["opt"][e]
     return sorted(range(len(ops)), key=lambda i: (best[1][i], i)), best[0]
+
+
+def guesses(T):
+    out = []; base = dict(COST)
+    for m in GUESS:
+        COST.update(m); ops = build(T, None); m = dict(COST); COST.update(base)
+        cost = [{e: c[1] for e, c in o["opt"].items()} if "opt" in o else {o["eng"]: o["cost"]} for o in ops]
+        out.append((m, cost, [o.get("lat", 0) for o in ops], [o.get("bytes", 0) for o in ops]))
+    return out
+
+
+def play(seq, eng, pred, guess, was, start):
+    m, cost, lat, size = guess
+    same, hop, wake, d0, d1, rate = m["SAME"], m["HOP"], m["WAKE"], m["D0"], m["D1"], m["RATE"]
+    end, fin = list(was[0]), list(was[1]); free = dict.fromkeys("VSPGYN", 0.0); ring = 0.0
+    for i in seq[:start]:
+        free[eng[i]] = end[i]
+        if size[i]:
+            ring = fin[i] - d1
+    for i in seq[start:]:
+        e = eng[i]; t = free[e]; w = wake if e == "G" else 0.0
+        for j in pred[i]:
+            x = fin[j] + (same if eng[j] == e else hop) + w
+            if x > t:
+                t = x
+        t += cost[i][e]; free[e] = end[i] = t
+        if size[i]:
+            ring = max(ring, t + d0) + size[i] / rate; fin[i] = ring + d1
+        else:
+            fin[i] = t + lat[i]
+    return end, fin
+
+
+def anneal(ops, seq, T):
+    n = len(ops); pred = [sorted(o["sdep"]) for o in ops]; succ = [[] for _ in ops]
+    for o in ops:
+        for j in pred[o["id"]]:
+            succ[j].append(o["id"])
+    eng = [o["eng"] for o in ops]; either = [i for i, o in enumerate(ops) if "opt" in o]; gs = guesses(T); x = [PAR["seed"]]
+
+    def rnd():
+        x[0] = (x[0] * 6364136223846793005 + 1442695040888963407) % (1 << 64)
+        return ((x[0] >> 11) + 1) / float((1 << 53) + 1)
+
+    now = [play(seq, eng, pred, g, ([0.0] * n, [0.0] * n), 0) for g in gs]
+    unit = [max(a[1]) for a in now]; cur = 1.0; best = (cur, seq, eng); steps = PAR["steps"]
+    for it in range(steps):
+        s, e = seq, eng
+        if it % 100 == 0:
+            k = it // 100 % len(gs); end, fin = now[k]; before = {}; last = {}
+            for i in seq:
+                before[i] = last.get(eng[i]); last[eng[i]] = i
+            i = fin.index(max(fin)); hot = []
+            while i is not None:
+                hot.append(i); b = before[i]
+                i = max(pred[i], key=lambda j: fin[j], default=None)
+                if b is not None and (i is None or end[b] > fin[i] + gs[k][0]["SAME"]):
+                    i = b
+            hot2 = [i for i in hot if "opt" in ops[i]] or either
+        aim = rnd() < PAR["aim"]
+        if rnd() < 0.15:
+            i = (hot2 if aim else either)[int(rnd() * len(hot2 if aim else either))]; q = p = seq.index(i); e = list(eng); e[i] = "V" if e[i] == "S" else "S"
+            near = [k for k in range(max(0, p - 25), min(n, p + 25)) if "opt" in ops[seq[k]] and eng[seq[k]] == e[i]]
+            if near and rnd() < 0.6:
+                q = near[int(rnd() * len(near))]; e[seq[q]] = eng[i]
+        else:
+            p = seq.index(hot[int(rnd() * len(hot))]) if aim else int(rnd() * n); i = seq[p]; lo, hi = max(0, p - 40), min(n, p + 41); pos = {seq[k]: k for k in range(lo, hi)}
+            far = int(-math.log(rnd()) / 0.7)
+            if rnd() < 0.5:
+                c = [k for k in range(max([pos[j] + 1 for j in pred[i] if j in pos] + [lo]), p) if eng[seq[k]] == eng[i]][::-1]
+            else:
+                c = [k for k in range(p + 1, min([pos[j] for j in succ[i] if j in pos] + [hi])) if eng[seq[k]] == eng[i]]
+            if not c or ops[i].get("load"):
+                continue
+            q = c[min(far, len(c) - 1)]
+            if ops[seq[q]].get("load"):
+                continue
+            s = seq[:q] + [i] + seq[q:p] + seq[p + 1:] if q < p else seq[:p] + seq[p + 1:q + 1] + [i] + seq[q + 1:]
+        room = -len(gs) * PAR["heat"] * 0.1 ** (it / steps) * math.log(rnd()); new = []; loss = 0.0
+        for g, a, u in zip(gs, now, unit):
+            new.append(play(s, e, pred, g, a, min(p, q))); loss += (max(new[-1][1]) - max(a[1])) / u
+            if loss > room + 0.002:
+                break
+        if loss <= room:
+            cur, seq, eng, now = cur + loss / len(gs), s, e, new
+            if cur < best[0]:
+                best = (cur, s, e)
+    return best[1], best[2]
+
+
+ORDER = []
+
+
+def arrange(T, send):
+    ops = build(T, send)
+    depend(ops)
+    if not ORDER:
+        ORDER.extend(anneal(ops, refine(ops)[0], T))
+    seq, eng = ORDER
+    for k, i in enumerate(seq):
+        o = ops[i]; o["t0"] = k
+        if "opt" in o:
+            o["eng"] = eng[i]; o["fns"] = o["opt"][eng[i]][0]
+    return ops, seq
 
 
 def rank_program(g, core, T, topo):
@@ -544,11 +771,9 @@ def rank_program(g, core, T, topo):
         q.remote_dma(out_ap, in_ap, T.sem[sem], T.sem["sent"], pid, rid, sum(1 << e for e in es))
         sent[0] += len(es)
 
-    ops = build(T, send)
-    depend(ops)
-    seq, _ = refine(ops)
+    ops, seq = arrange(T, send)
     queue = {"V": g.vector, "S": g.scalar, "P": g.tensor, "G": g, "Y": g.sync}
-    count = {e: 0 for e in "VSPG"}; known = {e: {} for e in "VSPGY"}; total = {}
+    count = {e: 0 for e in "VSPG"}; known = {e: {} for e in "VSPGY"}; total = {}; alone = [False]
     for i in seq:
         o = ops[i]; e = o["eng"]
         if e == "N":
@@ -562,6 +787,11 @@ def rank_program(g, core, T, topo):
                 q.wait_ge(T.sem[s], c); kn[s] = c
                 for s2, c2 in d["know"].items():
                     kn[s2] = max(kn.get(s2, 0), c2)
+        if e == "G" and not o.get("remote"):
+            part = o["w"][0][4] is not None
+            if (part or alone[0]) and kn.get("cG", 0) < count["G"]:
+                q.wait_ge(T.sem["cG"], count["G"]); kn["cG"] = count["G"]
+            alone[0] = part
         o["know"] = dict(kn)
         if o.get("remote"):
             o["fns"][0](q)
@@ -570,8 +800,9 @@ def rank_program(g, core, T, topo):
                 f(q).then_inc(T.sem[o["sem"]], 16)
             o["tok"] = (o["sem"], 16 * len(o["fns"])); total[o["sem"]] = o["tok"][1]
         else:
-            for f in o["fns"]:
-                f(q).then_inc(T.sem["c" + e], 1); count[e] += 1
+            for f in o["fns"][:-1]:
+                f(q)
+            o["fns"][-1](q).then_inc(T.sem["c" + e], 1); count[e] += 1
             o["tok"] = ("c" + e, count[e]); total["c" + e] = count[e]
     total["sent"] = sent[0]
     for s, c in total.items():

import math
from concourse.mybir import AluOpType, ActivationFunctionType

ALU = AluOpType
ACT = ActivationFunctionType
W, P, TV, H = 2048, 256, 3, 128
MD = 4
XW = W + 16
F32, BF, F16, I32, U16 = "float32", "bfloat16", "float16", "int32", "uint16"

SCRATCH = {
    "X0": ("sbuf", [128, W + 10 * H], BF), "X1": ("sbuf", [128, W + 10 * H], BF),
    "Q0": ("sbuf", [128, W + H], I32), "Q1": ("sbuf", [128, W + H], I32),
    "NUM": ("sbuf", [128, W + H], F32), "Y": ("sbuf", [128, 2 * W], F32), "Q16": ("sbuf", [128, W], F16), "Yc": ("sbuf", [128, P], F32),
    "x": ("sbuf", [128, 16 + 2 * XW], BF), "ab": ("sbuf", [128, 2 * 13 * H], BF), "am": ("sbuf", [128, 4096], F16),
    "Xc": ("sbuf", [128, 4096], BF), "Xb": ("sbuf", [128, 4096], F16), "mx": ("sbuf", [128, 2 * 17 * H], F16),
    "rp32": ("sbuf", [128, P], I32), "R0": ("sbuf", [128, P], U16), "R1": ("sbuf", [128, P], U16), "R2": ("sbuf", [128, P], U16),
    "O0": ("sbuf", [128, P], U16), "O1": ("sbuf", [128, P], U16), "Of": ("sbuf", [128, P], F32), "Rf": ("sbuf", [128, P], F32),
    "R16": ("sbuf", [128, P], F16), "s1": ("sbuf", [128, 208], I32), "ri": ("sbuf", [128, 16], I32),
    "ut": ("sbuf", [128, 16], I32), "uT": ("sbuf", [128, P], F16), "q8e": ("sbuf", [128, 8], BF),
    "rT": ("sbuf", [128, P], BF), "pl": ("sbuf", [128, 64], U16),
    "ur": ("sbuf", [128, 16], I32), "u": ("sbuf", [128, 16], I32), "uu": ("sbuf", [128, 16], F32),
    "z1": ("sbuf", [128, 320], I32), "z2": ("sbuf", [128, 320], I32), "CL": ("sbuf", [128, 320], I32), "cl": ("sbuf", [128, 288], U16),
    "bl": ("sbuf", [128, P], U16), "Hh": ("sbuf", [128, P], F32),
    "s2": ("sbuf", [128, 272], I32), "twi": ("sbuf", [128, 16], I32), "tT": ("sbuf", [128, P], BF),
    "cwf": ("sbuf", [128, 288], I32), "cwi": ("sbuf", [128, 16], I32), "cw": ("sbuf", [128, 16], U16),
    "Qw": ("sbuf", [128, P], F32), "t1": ("sbuf", [128, P], F32), "t3": ("sbuf", [128, P], I32), "t4": ("sbuf", [128, P], I32),
    "S2": ("sbuf", [128, P], I32), "m1": ("sbuf", [128, P], F16), "m2": ("sbuf", [128, P], I32), "m16": ("sbuf", [128, P], F16),
    "ys": ("sbuf", [128, P], F32), "sg": ("sbuf", [128, 16], BF), "aj": ("sbuf", [128, 16], F32), "Acol": ("sbuf", [128, 4], F32),
    "wk": ("sbuf", [128, 16], I32), "col": ("sbuf", [128, 24], F32), "pI": ("sbuf", [128, 8], I32),
    "D0": ("sbuf", [128, 128], F32), "KK": ("sbuf", [128, 128], BF), "G16": ("sbuf", [128, 128], BF), "C144": ("sbuf", [128, 144], BF),
    "t18": ("sbuf", [128, 144], BF), "q18": ("sbuf", [128, 144], BF), "e18": ("sbuf", [128, 432], BF), "sm": ("sbuf", [128, 128], F32), "smi": ("sbuf", [128, 16], I32),
    "Ib": ("sbuf", [128, 128], BF), "nI": ("sbuf", [128, 128], BF), "I32": ("sbuf", [128, 128], BF), "BLK": ("sbuf", [128, 128], BF),
    "ones": ("sbuf", [128, 128], BF), "I2": ("sbuf", [128, 128], BF), "b8": ("sbuf", [128, 48], BF),
    "Sel": ("sbuf", [128, 144], BF), "Wsel": ("sbuf", [128, 288], BF), "LBb": ("sbuf", [128, 144], BF),
    "LBf": ("sbuf", [128, 144], F32), "LBa": ("sbuf", [128, 288], BF), "db": ("sbuf", [128, 128], BF),
    "L1": ("sbuf", [128, 64], F16), "Z1": ("sbuf", [128, 144], BF), "Z2": ("sbuf", [128, 144], BF), "Z3": ("sbuf", [128, 8], BF),
    "kd": ("sbuf", [128, 288], F16), "KapT": ("sbuf", [128, 288], F32), "lists": ("sbuf", [128, 32], U16),
    "c1": ("sbuf", [128, 104], F32), "c2": ("sbuf", [128, 136], F32), "zc": ("sbuf", [128, 160], F32), "tm": ("sbuf", [128, 16], F32),
    "FH": ("sbuf", [128, 128], BF), "FW": ("sbuf", [128, 128], F16), "Ff": ("sbuf", [128, 128], F32),
}
for _b in range(8):
    SCRATCH["p%d" % _b] = ("psum", [128, 32, 16] if _b < 4 else [128, 512], F32)
DMAS = [a + str(h) for a in ("lx", "lr", "lq", "lw", "lk", "oq", "ox", "or", "yc", "ex0", "ex1", "eq0", "eq1") for h in range(2)]
SEMAPHORES = ["cV", "cS", "cP", "cG", "sent"] + DMAS + ["ar%d%d" % (v, h) for v in range(TV) for h in range(2)]

COST = {"CY": 1.0, "GA": 1.5, "SC": 3.5, "PE": 0.5, "PF": 0.0, "TT2": 1.0, "HOP": 120.0, "SAME": 70.0, "LINK": 2800.0, "GX": 1.5, "GA0": 100.0, "FIRST": 3000.0}
WIDTH = {F32: 4, I32: 4, BF: 2, F16: 2, U16: 2}
PAR = {"t4": 0, "ut": 0, "n3": 0, "dq": 1, "de": 1, "os": 1, "su": 1, "num": 1024, "b": ["VVVV"] * 6, "jb": 3, "ns": 2, "nx": 4, "nc": 4, "sint": 1, "m1": "V", "walk": 1, "look": 310.0, "fill": 120.0, "dup": "GG",
       "rounds": 1, "vpen": 100.0, "key": None}
PAR["lead"] = {'x00': 39, 'j00': 185, 'a00': 89, 'p00': -95, 'r00': 36, 'e00': 65, 'w00': 44, 's00': -14, 'x01': -38, 'j01': -21, 'a01': 5, 'p01': -224, 'r01': 0, 'e01': -2, 'w01': 28, 's01': 39, 'x10': 41, 'j10': 43, 'a10': 103, 'p10': -112, 'r10': 11, 'e10': 39, 'w10': 19, 's10': -14, 'x11': 27, 'j11': 44, 'a11': -5, 'p11': -104, 'r11': -11, 'e11': -61, 'w11': -129, 's11': -115, 'x20': 85, 'j20': 103, 'a20': 119, 'p20': -16, 'r20': 64, 'e20': 18, 'w20': 55, 's20': -147, 'x21': 0, 'j21': 15, 'a21': 86, 'p21': -204, 'r21': 2, 'e21': 3, 'w21': 103, 's21': -50, 'g00': 44, 'c00': 114, 'y20': -181, 'y21': -40}
PAR.update(look=350.0, fill=150.0, vpen=100.0, num=2048, n3=0, dq=0, de=0, os=0, su=0, nc=4, jb=3, ns=2, m1="S", ut=0, b=["SSSS"] * 6, t4=1)
PAR.update(aim=0.4, fx=0, steps=110000, heat=0.0003, seed=1, nc=2, su=0, num=2048)
PAR["lead"] = dict({p + str(v) + "0": 40 for v in range(TV) for p in "xjapyrews"}, g00=60, c00=150)
COST.update(CY=1.0, GA=1.5, SC=3.5, PE=.5, PF=0.0, PM=64, HOP=120., SAME=70., LINK=2600., FIRST=500., GX=1.4, GA0=80., TG=0.0, SF=0.0, SX=1.0,
            SEND=500.0, ISSUE=60.0, WAKE=200.0, D0=1200.0, D1=700.0, RATE=400.0)
SIZE = {"lx": 512, "lq": 1024, "lr": 64, "lw": 8, "lk": 8, "ex": 256, "eq": 512, "yc": 64, "oq": 32, "ox": 32, "or": 64}
GUESS = [dict(CY=1.04, GA=1.55, PE=.52, GX=1.3, GA0=0.0),
         dict(CY=1.01, GA=1.27, PE=.45, SAME=50., LINK=1700., SEND=200., SF=22., SX=1.12, TG=2.0, TT2=2.0, RATE=600., GX=1.2, GA0=0.0),
         dict(CY=.95, GA=1.57, PE=.4, SAME=160., LINK=1500., SF=40., SX=1.12, WAKE=0.0, RATE=490., D1=400., GX=1.0, GA0=0.0),
         dict(CY=.93, GA=1.6, SC=2.8, PE=.47, PF=5., HOP=70., SAME=110., LINK=3200., SEND=1000., FIRST=1500., SF=40., TG=2.0, RATE=330., D0=1600.,
              GX=1.6, GA0=0.0),
         dict(CY=.92, GA=1.35, SC=3.5, PE=.76, HOP=110., SAME=80., LINK=2200., SEND=500., FIRST=800., SF=30., TG=1.8, RATE=450., D0=1300.,
              WAKE=300., GX=1.4, GA0=0.0)]


def build(T, send):
    ops = []
    CY, GA, SC, PE = COST["CY"], COST["GA"], COST["SC"], COST["PE"]
    tag = [0, 0, "c"]

    def v(name, lo=0, hi=None, st=1, a=None):
        return (name, lo, SCRATCH[name][1][1] if hi is None else hi, st, a)

    def rows(a):
        return slice(0, 128) if a is None else slice(64 * a, 64 * a + 64)

    def ap(a):
        if isinstance(a, tuple) and a[0] == "ind":
            return ap(a[1]).indirect(ap(a[2]))
        if isinstance(a, tuple) and len(SCRATCH[a[0]][1]) == 3:
            k = a[1] % 16 if a[3] == 16 else slice(*a[5]) if len(a) > 5 else slice(0, 16)
            return T[a[0]][:, a[1] // 16:a[2] // 16, k]
        if isinstance(a, tuple):
            return T[a[0]][rows(a[4]), a[1]:a[2]:a[3]] if a[3] != 1 else T[a[0]][rows(a[4]), a[1]:a[2]]
        return a

    def ind(win, off):
        return ("ind", win, off)

    def views(xs):
        out = []
        for a in xs:
            if isinstance(a, tuple):
                out += [a[1], a[2]] if a[0] == "ind" else [a]
        return out

    def n_of(a):
        if a[0] == "ind":
            return 16 * (a[2][2] - a[2][1])
        if len(a) > 5:
            return (a[2] - a[1]) // 16 * (a[5][1] - a[5][0])
        return (a[2] - a[1] + a[3] - 1) // a[3]

    def add(eng, fns, outs, ins, cost, **kw):
        w, r = [], views(ins)
        for o in outs:
            if o[0] == "ind":
                w.append(o[1]); r.append(o[2])
            else:
                w.append(o)
        d = {"eng": eng, "fns": fns, "w": w, "r": r, "cost": cost, "vis": tag[0], "half": tag[1], "ph": tag[2]}
        d.update(kw)
        ops.append(d)
        return d

    def vcost(out, ins, tt=False):
        n = n_of(out)
        if out[0] == "ind":
            return 50 + 16 * (out[2][2] - out[2][1]) * SC * CY
        if ins[0][0] == "ind":
            return 50 + n * max(GA, COST.get("TG", 0) if tt else 0) * CY
        two = all(WIDTH[SCRATCH[a[0]][2]] == 2 for a in views([out] + ins))
        c = 1.0
        if tt and not any(SCRATCH[a[0]][0] == "psum" for a in views(ins)):
            c = COST["TT2"] if two else 2.0
        elif two:
            c = 0.5
        return max(64, n * c) * CY

    def cp(out, in_):
        return add("V", [lambda q: q.tensor_copy(ap(out), ap(in_))], [out], [in_], vcost(out, [in_]))

    def tt(out, a, b, op):
        return add("V", [lambda q: q.tensor_tensor(ap(out), ap(a), ap(b), op)], [out], [a, b], vcost(out, [a, b], True))

    def ts(out, a, s1, op0, s2=None, op1=None):
        if op1 is None:
            f = lambda q: q.tensor_scalar(ap(out), ap(a), ap(s1), None, op0)
        else:
            f = lambda q: q.tensor_scalar(ap(out), ap(a), ap(s1), ap(s2), op0, op1)
        return add("V", [f], [out], [a, s1, s2], vcost(out, [a]))

    def scan(out, d0, d1, op0, op1):
        return add("V", [lambda q: q.tensor_tensor_scan(ap(out), ap(d0), ap(d1), 0.0, op0, op1)], [out], [d0, d1], max(64, n_of(out)) * CY)

    def ms(out, c):
        return add("V", [lambda q: q.memset(ap(out), c)], [out], [], max(64, n_of(out) * WIDTH[SCRATCH[out[0]][2]] / 4) * CY)

    def act(out, in_, func, bias=None, scale=None, acc=None):
        kw = {}
        if bias is not None: kw["bias"] = bias
        if scale is not None: kw["scale"] = scale
        if acc is not None: kw["accum_out"] = acc
        f = lambda q: q.activation(ap(out), ap(in_), func, **{k: ap(a) for k, a in kw.items()})
        n = n_of(out)
        return add("S", [f], [out] + ([acc] if acc else []), [in_, bias, scale],
                   COST.get("SF", 0) + (65 + n * GA * CY * COST.get("SG", 1) if in_[0] == "ind" else max(64, n) * CY * COST.get("SX", 1)))

    def gather(out, in_, scale=None):
        a = cp(out, in_) if scale is None else ts(out, in_, scale, ALU.mult)
        ops.pop()
        b = act(out, in_, ACT.Copy, scale=scale)
        b["opt"] = {"S": (b["fns"], b["cost"]), "V": (a["fns"], a["cost"])}
        return b

    def affine(out, in_, scale, bias):
        a = ts(out, in_, scale, ALU.mult, bias, ALU.add)
        if not PAR["sint"]:
            return a
        ops.pop()
        b = act(out, in_, ACT.Identity, scale=scale, bias=bias)
        b["opt"] = {"S": (b["fns"], b["cost"]), "V": (a["fns"], a["cost"])}
        return b

    def mm(groups, first=True, last=True):
        fns, outs, ins, cost = [], [], [], 0.0
        for out, terms in groups:
            outs.append(out)
            for i, t in enumerate(terms):
                l, r, o = t[0], t[1], t[2] if len(t) > 2 else out
                fns.append(lambda q, o=o, l=l, r=r, a=(first and i == 0), z=(last and i == len(terms) - 1): q.matmul(ap(o), ap(l), ap(r), a, z))
                ins += [l, r]
                cost += COST.get("PF", 0) + max(min(COST.get("PM", 64), n_of(l)), n_of(r)) * PE * (4 if SCRATCH[l[0]][2] == F32 else 1)
        return add("P", fns, outs, ins, cost, goes_on=not first)

    def iota(out, pattern, base, cm):
        if SCRATCH[out[0]][2] == I32:
            f = lambda q: q.iota(ap(out), pattern, base, cm)
        else:
            f = lambda q: q.iota(ap(out), pattern, base, cm, allow_small_or_imprecise_dtypes=True)
        return add("G", [f], [out], [], COST["GX"] * (130 + 2 * n_of(out) * CY) + COST["GA0"])

    def keep(out, in_, pattern, op, fill, base, cm):
        return add("G", [lambda q: q.affine_select(ap(out), ap(in_), pattern, op, fill, base, cm)], [out], [in_],
                   COST["GX"] * (170 + 2 * n_of(out) * CY) + COST["GA0"])

    def gcopy(out, in_):
        return keep(out, in_, [[0, n_of(out)]], ALU.is_ge, 0.0, 0, 0)

    def dma(eng, sem, f, outs, ins, lat, n=2):
        return add(eng, [lambda q, a=a: q.dma_start(*f(a)) for a in range(n)], outs, ins, COST["ISSUE"] * n, sem=sem, lat=lat,
                   bytes=1024 * SIZE[sem[:2]], load=sem[0] == "l")

    eq, ne, ge, mul, sub, addo, mn, mxo, band = (ALU.is_equal, ALU.not_equal, ALU.is_ge, ALU.mult, ALU.subtract, ALU.add, ALU.min, ALU.max,
                                                 ALU.bitwise_and)
    shr = ALU.arith_shift_right
    Xs, Qs = [v("X%d" % h, 0, W) for h in range(2)], [v("Q%d" % h, 0, W) for h in range(2)]
    K = W // 2

    def hv(name, h, n=H, lo=0, hi=None, st=1, a=None):
        return v(name, h * n + lo, h * n + (n if hi is None else hi), st, a)

    def xv(h, lo, hi, st=1):
        return v("x", 16 + XW * h + lo, 16 + XW * h + hi, st)

    for h in range(2):
        dma("S", "lr%d" % h, lambda a, h=h: (T.rp32[rows(a), H * h:H * h + H], T.rp[rows(h), H * a:H * a + H]), [v("rp32", H * h, H * h + H)], [], 2200)
        dma("Y", "lx%d" % h, lambda a, h=h: (T["X%d" % h][rows(a), 0:W], T.xf[rows(h), :]), [Xs[h]], [], 3200 + 1800 * h)
    for h in range(2):
        dma("Y", "lw%d" % h, lambda a, h=h: (T.wk[rows(a), 4 * h:4 * h + 1], T.wt[rows(h), :]), [v("wk", 4 * h, 4 * h + 4)], [], 5000)
        dma("Y", "lk%d" % h, lambda a, h=h: (T.wk[rows(a), 8 + 4 * h:9 + 4 * h], T.kap[rows(h), :]), [v("wk", 8 + 4 * h, 12 + 4 * h)], [], 5000)
    for h in range(2):
        dma("Y", "lq%d" % h, lambda a, h=h: (T["Q%d" % h][rows(a), 0:W], T.pa[rows(h), :]), [Qs[h]],
            [Xs[0], Qs[0]][:1 + h] if PAR["dq"] else [], 6000 - 1500 * h if PAR["dq"] else 9000 + 4000 * h)

    iota(v("D0"), [[1, 128]], 0, -1)
    iota(v("pI", 0, 1), [[0, 1]], 0, 1)
    iota(v("sm", 0, 32), [[0, 4], [1, 8]], 0, 0)
    iota(v("KK"), [[0, 8], [1, 16]], 0, 0)
    iota(v("sm", 32, 40), [[0, 8]], 13, 16)
    iota(v("sm", 40, 56), [[2, 2], [0, 8]], 12, 16)
    iota(v("sm", 56, 64), [[0, 8]], W + 14, 0)
    iota(v("C144"), [[1, 144]], -15, 0)
    iota(v("sm", 64, 73), [[16, 9]], 0, 0)
    iota(v("sm", 80, 88), [[2, 8]], 2, 0)
    iota(v("t18"), [[0, 8], [1, 18]], -2, 0)
    Ib, nI, db, BLK = v("Ib"), v("nI"), v("db"), v("BLK")
    ts(Ib, v("D0"), 0.0, eq)
    act(nI, Ib, ACT.Copy, scale=-1.0); act(v("I32"), Ib, ACT.Copy, scale=1.0 / 32); act(v("I2"), Ib, ACT.Copy, scale=2.0)
    for j, (s, o) in enumerate(((15, band), (4, shr), (7, band), (6, shr))):
        ts(v("pI", j + 1, j + 2), v("pI", 0, 1), s, o)
    ts(v("pI", 5, 6), v("pI", 0, 1), 15, band, 3, shr)
    cp(v("col", 0, 6), v("pI", 0, 6))
    pr, pq, p7, p64, p3 = (v("col", j, j + 1) for j in (1, 2, 3, 4, 5))
    p16, pr1, yb, pc, pr8, pr8k = (v("col", j, j + 1) for j in (6, 7, 8, 9, 10, 11))
    act(p16, pq, ACT.Copy, scale=16.0); act(pr1, pr, ACT.Identity, bias=1.0); act(pr8, pr, ACT.Copy, scale=8.0)
    act(pr8k, p64, ACT.Identity, scale=float(K), bias=pr8)
    ts(yb, pr, 1.0, eq, -1024.0 * 136, mul)
    act(pc, p7, ACT.Identity, scale=18.0, bias=p3)
    cp(v("col", 12, 14), v("wk", 0, 8, 4)); cp(v("col", 14, 16), v("wk", 8, 16, 4))
    wc, kc = [v("col", 12 + h, 13 + h) for h in range(2)], [v("col", 14 + h, 15 + h) for h in range(2)]
    q8 = v("sm", 0, 8)
    b16, bm32 = v("b8", 0, 8), v("b8", 8, 16)
    ts(b16, q8, pq, eq, 16.0, mul)
    act(bm32, b16, ACT.Copy, scale=-2.0)
    if PAR["ut"]:
        act(v("q8e"), b16, ACT.Copy, scale=1.0 / 16)
    ms(v("c1"), 1.0); ms(v("c1", 0, 104, 13), -1.0e6); ms(v("c2"), 1.0); ms(v("c2", 0, 136, 17), -1.0e6)
    ms(v("zc"), 1.0); ms(v("zc", 0, 144, 18), 0.0); ms(v("zc", 1, 144, 18), 0.0); ms(v("zc", 144, 160, 2), 0.0)
    ms(v("Acol", 0, 1), -0.484375); ms(v("x", 0, 16), 0.0)
    bc16, bcq, perm = v("lists", 0, 8), v("lists", 8, 17), v("lists", 18, 27)
    cp(bc16, q8)
    ts(db, v("KK"), pr, eq)
    ts(v("L1", 0, 32), v("sm", 0, 32), pq, eq, -1.0, mul)
    ts(v("sm", 96, 128), v("sm", 0, 32), pq, eq)
    tt(v("L1", 32, 64), v("sm", 96, 128), v("sm", 32, 64), mul)
    ts(v("Sel"), v("C144"), p16, eq)
    act(v("tm", 0, 9), v("sm", 64, 73), ACT.Identity, bias=pr)
    ts(v("smi", 0, 9), v("tm", 0, 9), 1.0 / 18, mul, 0.5 / 18 - 0.5, addo); cp(bcq, v("smi", 0, 9))
    ts(v("lists", 18, 26), v("sm", 80, 88), pc, addo); ts(v("lists", 26, 27), p7, 2.0, mul, 145.0, addo)
    ms(v("ones"), 1.0)
    iota(v("G16"), [[16, 8], [0, 16]], 0, 0); ts(BLK, v("G16"), p16, eq)
    ts(v("e18", 0, 144), v("t18"), pr, eq); ts(v("e18", 144, 288), v("t18"), pr1, eq)
    tt(v("e18", 288, 432), v("e18", 0, 144), v("e18", 144, 288), sub)
    for h in range(2):
        ts(xv(h, W, W + 16), v("KK", 0, 16), -2.0, addo, pr, eq)
        if PAR["ut"]:
            act(hv("Wsel", h, 144, 0, 8), v("q8e"), ACT.Copy, scale=wc[h])
        else:
            act(hv("Wsel", h, 144), v("Sel"), ACT.Copy, scale=wc[h])
        act(hv("kd", h, 144), v("e18", 288, 432), ACT.Copy, scale=kc[h])
        mm([(v("p%d" % (6 + h), 0, 144), [(BLK, hv("kd", h, 144))])])
        act(hv("KapT", h, 144), v("p%d" % (6 + h), 0, 144), ACT.Copy)
        ts(hv("z1", h, 160, 144, 160, 2), q8, 128.0, mul, pr8k, addo)
    tag[2] = "g"
    FH, FW, Ff = v("FH"), v("FW"), v("Ff")
    D = [[1, 128]]
    iota(FH, [[0, 128]], 0, 0); keep(FH, FH, D, ge, -128.0, -3, -1); keep(FH, FH, D, ne, 4096.0, -1, -1); tt(FH, FH, BLK, mul)
    iota(Ff, [[0, 8], [-37, 16]], 0, 0); keep(FW, Ff, D, ge, 0.0, -3, -1); keep(FW, FW, D, ge, 8192.0, -1, -1)
    keep(FW, FW, D, ne, -8192.0, -1, -1); tt(FW, FW, BLK, mul)
    Z1, Z2, Z3, q18, S18 = v("Z1"), v("Z2"), v("Z3"), v("q18"), [[0, 8], [1, 18]]
    iota(q18, [[1, 8], [0, 18]], 0, 0); keep(Z1, q18, S18, ge, -1.0, -2, 0); ts(Z1, Z1, pq, eq, 8192.0, mul)
    iota(Z2, [[0, 8], [8192, 18]], -8192 * 17 - 4096, 0); keep(Z2, Z2, S18, ne, -4194304.0, 0, 0); keep(Z2, Z2, S18, ne, float(W), -1, 0)
    ts(q18, q18, pq, eq); tt(Z2, Z2, q18, mul)
    ts(Z3, q8, pq, eq, v("col", 0, 1), mul)
    n = PAR["num"]
    iota(v("NUM", 0, n), [[1, n]], 0, 0); iota(v("NUM", W), [[0, H]], 0, 0)
    for c in range(n, W, 512):
        act(v("NUM", c, c + 512), v("NUM", 0, 512), ACT.Identity, bias=float(c))
    act(v("LBb"), v("Sel"), ACT.Copy, scale=pr1)
    tag[:] = [1, 0, "g"]
    gcopy(v("LBf"), v("LBb"))["late"] = True
    keep(v("LBa", 0, 144), v("LBb"), [[0, 144]], ge, 0.0, 63, -1)["late"] = True
    keep(v("LBa", 144, 288), v("LBb"), [[0, 144]], ge, 0.0, -64, 1)["late"] = True
    tag[:] = [0, 0, "c"]
    cp(v("R0", 0, H), v("rp32", 0, H)); cp(v("R0", H, P), v("rp32", H, P))

    def sel(name, r, lo=0, a=None):
        return v(name, lo + 15 - r, lo + 143 - r, 1, a)

    fcp = gather if PAR["fx"] else cp
    big = [0, 0]

    def bank(h):
        big[h] += 1
        return "p%d" % (2 * h + big[h] % 2)

    X1, MK = (5, 6) if PAR["n3"] else (2, 3)

    def near(h, j, n=1):
        return v("X%d" % h, W + j * H, W + (j + n) * H)

    def jumps(vis, h):
        tag[:] = [vis, h, "x"]
        R, pv, ps, X = "R%d" % vis, "p%d" % (4 + h), "p%d" % (6 + h), Xs[h]
        n = PAR["nx"]
        for j in range(n):
            gather(xv(h, W // n * j, W // n * (j + 1)), ind(X, hv(R, h, H, H // n * j, H // n * (j + 1))))
        tag[2] = "j"
        if PAR["jb"] == 3:
            for j in range(4):
                b = v(bank(h), 0, 512)
                mm([(b, [(Ib, xv(h, 512 * j, 512 * j + 512)), (nI, xv(h, 512 * j - 1, 512 * j + 511))])])
                act(hv("ab", h, 13 * H, 416 * j, 416 * j + 416), b + ((2, 15),), ACT.Abs)
            mm([(v(pv, k, 104, 13), [(hv("ab", h, 13 * H, k, None, 13), b16)]) for k in range(13)])
        elif PAR["jb"] == 1:
            xk = lambda k: xv(h, k, W, 16)
            for ks in (range(1, 5), range(5, 8), range(8, 11), range(11, 14)):
                ak = lambda k, n=1: hv("ab", h, 13 * H, H * (k - 1), H * (k - 1 + n))
                b = bank(h)
                mm([(v(b, H * j, H * j + H), [(Ib, xk(k + 1)), (nI, xk(k))]) for j, k in enumerate(ks)])
                act(ak(ks[0], len(ks)), v(b, 0, H * len(ks)), ACT.Abs)
                mm([(v(pv, k - 1, 104, 13), [(ak(k), b16)]) for k in ks])
        else:
            for a, ks in ((a, ks) for a in range(2) for ks in (range(1, 8), range(8, 14))):
                xk = lambda k: xv(h, K * a + k, K * a + K, 16)
                ak = lambda k, n=1: hv("ab", h, 13 * H, 64 * (13 * a + k - 1), 64 * (13 * a + k - 1 + n))
                b = bank(h)
                mm([(v(b, 64 * j, 64 * j + 64), [(Ib, xk(k + 1)), (nI, xk(k))]) for j, k in enumerate(ks)])
                act(ak(ks[0], len(ks)), v(b, 0, 64 * len(ks)), ACT.Abs)
                mm([(v(pv, k - 1, 104, 13, a), [(ak(k), b16)]) for k in ks])
        tag[2] = "a"
        scan(hv("s1", h, 104), v("c1"), v(pv, 0, 104), addo, mxo)
        ts(hv("ri", h, 8), hv("s1", h, 104, 12, None, 13), 15, band)
        tt(hv("rT", h), ind(hv("ri", h, 8), bc16), db, mul)
        mm([(v(pv, 104, 136), [(db, v("L1", 32, 64)), (hv("rT", h), v("L1", 0, 32))])])
        (gather if PAR["su"] else cp)(hv("pl", h, 32), v(pv, 104, 136))
        gather(near(h, 0), ind(xv(h, 0, W + 16), hv("pl", h, 32, 0, 8)))
        if X1 == 2:
            gather(near(h, 1, 3), ind(xv(h, 0, W + 16), hv("pl", h, 32, 8, 32)))
        else:
            gather(near(h, X1, 2), ind(xv(h, 0, W + 16), hv("pl", h, 32, 16, 32)))
            gather(near(h, 1), ind(xv(h, 0, W + 16), hv("pl", h, 32, 8, 16)))
        for n in (1, 2):
            if n < MD:
                fcp(near(h, MK + n, n), near(h, MK, n))
        if "V" in PAR["b"][2 * vis + h]:
            for n in (1, 2):
                cp(near(h, X1 + 1 - 2 * n, n), near(h, X1 + 1 - n, n))
        u = hv("u", h, 8)
        if PAR["ut"]:
            mm([(v(pv, 136, 144), [(near(h, 0), hv("Wsel", h, 144, 0, 8))])])
            cp(hv("ur", h, 8), v(pv, 136, 144))
            ts(hv("ut", h, 8), hv("ur", h, 8), W - 1, band)
            tt(hv("uT", h), ind(hv("ut", h, 8), bc16), db, mul)
            mm([(v(pv, 408, 416), [(hv("uT", h), v("q8e"))])])
            cp(u, v(pv, 408, 416))
        else:
            mm([(v(pv, 136, 144), [(sel("Wsel", r, 144 * h), v(X[0], W + r, W + H, 16)) for r in range(16)])])
            fcp(hv("ur", h, 8), v(pv, 136, 144))
            ts(u, hv("ur", h, 8), W - 1, band)
        tt(hv("z1", h, 160, 0, 144), ind(u, bcq), hv("KapT", h, 144), mul)
        a = tt(hv("uu", h, 8), u, u, mul)
        if PAR["fx"]:
            ops.pop(); b = act(hv("uu", h, 8), u, ACT.Square); b["opt"] = {"S": (b["fns"], b["cost"]), "V": (a["fns"], a["cost"])}
        ts(hv("z1", h, 160, 145, 160, 2), u, 7, band)
        if PAR["fx"]:
            affine(hv("z1", h, 160, 1, 144, 18), hv("uu", h, 8), 1.0 / 32, v("Acol", vis, vis + 1))
        else:
            ts(hv("z1", h, 160, 1, 144, 18), hv("uu", h, 8), 1.0 / 32, mul, v("Acol", vis, vis + 1), addo)
        scan(hv("z2", h, 160), v("zc"), hv("z1", h, 160), mul, addo)
        ts(hv("CL", h, 160), hv("z2", h, 160), W - 1, band)
        cp(hv("cl", h, 144), ind(hv("CL", h, 160), perm))
        tag[2] = "p"
        (gather if PAR["t4"] else cp)(hv("R16", h), hv(R, h))
        affine(v("Q%d" % h, W), hv("R16", h), 1.0, 8192.0)
        mm([(v(ps, 0, H), [(v("I32"), hv("R16", h)), (FH, near(h, MK))]), (v(ps, H, 2 * H), [(nI, hv("R16", h)), (FW, near(h, MK))])])
        ts(hv("Hh", h), v(ps, 0, H), 0.0, mxo, 2049.0, mn)
        ts(v(ps, H, 2 * H), v(ps, H, 2 * H), -4096.484375, mxo, -2047.515625, addo)
        mm([(v(ps, 256, 400), [(db, Z2), (db, Z3, v(ps, 257, 400, 18))])], last=False)

    def sums(h):
        tag[:] = [TV - 1, h, "y"]
        for a in range(2):
            gcopy(hv("Q16", h, K, a=a), v("Q%d" % h, K * a, K * a + K, 1, a))["late"] = True
        b = bank(h)
        mm([(v(b, 0, H), [(sel("LBa", 2 * j + 1, 144 * a), v("X%d" % h, K * a + H * j, K * a + H * j + H)) for j in range(8) for a in range(2)]
             + [(sel("LBb", 2 * j), hv("Q16", h, K, H * j, H * j + H)) for j in range(8)])])
        gather(hv("Yc", h), v(b, 0, H))
        dma("Y", "yc%d" % h, lambda i: (T.Y[64 * (i // 2) + i % 2:64 * (i // 2) + 64:16, W * h + K * (i // 2):W * h + K * (i // 2) + K],
                                        T.Yc[64 * (i // 2) + i % 2:64 * (i // 2) + 64:2, H * h:H * h + H]), [hv("Y", h, W)], [hv("Yc", h)], 2400, 4)

    def stores(vis, h):
        tag[:] = [vis, h, "s"]
        for name, tab, src, lat in (("x", Xs[h], "m2", 2400), ("q", Qs[h], "S2", 3000)):
            cp(ind(tab, hv("cl", h, 144, H, H + 8)), hv(src, h))
            dma("Y", "e%s%d%d" % (name, vis, h), lambda a, t=tab[0]: (T[t][rows(1 - a), K * a:K * a + K], T[t][rows(a), K * a:K * a + K]),
                [tab], [tab, Xs[h]] if PAR["de"] else [tab], lat)

    def rivals(vis, h):
        tag[:] = [vis, h, "r"]
        pv, X, Q = "p%d" % (4 + h), Xs[h], Qs[h]
        n = PAR["nc"]
        for j in range(n):
            gather(hv("Xc", h, W, W // n * j, W // n * (j + 1)), ind(X, hv("cl", h, 144, H // n * j, H // n * (j + 1))), 2.0)
        n = PAR["ns"]; c = H // n
        for j in range(n):
            for m in range(16 // n * j, 16 // n * (j + 1), MD):
                tt(hv("am", h, W, H * m, H * (m + MD)), ind(Q, hv("cl", h, 144, 8 * m, 8 * (m + MD))), near(h, MK, MD), mul)
            mm([(v(pv, 144 + c * j, 144 + c * j + c), [(sel("Sel", r), hv("am", h, W, 16 * c * j + r, 16 * c * (j + 1), 16)) for r in range(16)])])
            (gather if PAR["su"] else cp)(hv("bl", h, H, c * j, c * j + c), v(pv, 144 + c * j, 144 + c * j + c))
            for i in range(4 // n * j, 4 // n * (j + 1)):
                o, w = hv("Xb", h, W, 512 * i, 512 * i + 512), ind(X, hv("bl", h, H, 32 * i, 32 * i + 32))
                if PAR["b"][2 * vis + h][i] == "V":
                    tt(o, w, near(h, X1 - 3, 4), addo)
                else:
                    gather(o, w)

    def scores(vis, h):
        tag[:] = [vis, h, "e"]
        pv = "p%d" % (4 + h)
        ot = lambda t, n=1: hv("mx", h, 17 * H, H * t, H * (t + n))
        b = bank(h)
        mm([(v(b, 0, H), [(v("I2"), near(h, 0)), (nI, near(h, 1)), (nI, near(h, X1))])])
        act(ot(0), v(b, 0, H), ACT.Abs)
        mm([(v(pv, 272, 408, 17), [(ot(0), bm32)])])
        for j in range(4):
            b = v(bank(h), 0, 512); c, xb = (hv(a, h, W, 512 * j, 512 * j + 512) for a in ("Xc", "Xb"))
            if PAR["b"][2 * vis + h][j] == "V":
                mm([(b, [(Ib, c)])], last=False)
            elif "V" in PAR["b"][2 * vis + h]:
                mm([(b, [(Ib, c), (nI, near(h, X1 - 3, 4))])], last=False)
            else:
                mm([(b, [(Ib, c)] + [(nI, near(h, X1), v(b[0], H * i, H * i + H)) for i in range(4)])], last=False)
            mm([(b, [(nI, xb)])], first=False)
            act(ot(4 * j + 1, 4), b, ACT.Abs)
            mm([(v(pv, 272 + t, 408, 17), [(ot(t), bm32)]) for t in range(4 * j + 1, 4 * j + 5)])

    def splice(vis, h):
        tag[:] = [vis, h, "w"]
        pv, ps = "p%d" % (4 + h), "p%d" % (6 + h)
        scan(hv("s2", h, 136), v("c2"), v(pv, 272, 408), addo, mxo)
        ts(hv("twi", h, 8), hv("s2", h, 136, 16, None, 17), 31, band)
        tt(hv("tT", h), ind(hv("twi", h, 8), bc16), db, mul)
        mm([(v(ps, 256, 400), [(hv("tT", h), Z1)])], first=False)
        scan(hv("cwf", h, 144), v(ps, 256, 400), hv("CL", h, 160, 0, 144), addo, mxo)
        cw = hv("cw", h, 8)
        ts(hv("cwi", h, 8), hv("cwf", h, 144, 17, None, 18), 2 * W - 1, band)
        fcp(cw, hv("cwi", h, 8))
        tt(hv("t1", h), ind(v("NUM"), cw), hv("Hh", h), mul)
        if PAR["t4"]:
            gather(hv("Qw", h), ind(v("Q%d" % h), cw))
            tt(v(ps, H, 2 * H), hv("t1", h), v(ps, H, 2 * H), sub)
            tt(hv("t4", h), hv("Qw", h), v(ps, H, 2 * H), mxo)
        else:
            tt(hv("t3", h), hv("t1", h), v(ps, H, 2 * H), sub)
            tt(hv("t4", h), ind(v("Q%d" % h), cw), hv("t3", h), mxo)
        ts(hv("S2", h), hv("t4", h), W - 1, band)
        last = vis == TV - 1
        src, dst = ("Of", "Rf") if last else ("O%d" % vis, "R%d" % (vis + 1))
        fcp(hv(src, h), hv("S2", h))
        s = add("G", [lambda q: send(q, ap(hv(dst, h)), ap(hv(src, h)), "ar%d%d" % (vis, h), last)], [], [hv(src, h)],
                COST["SEND"] + COST["FIRST"] * (vis + h == 0), remote=True)
        add("N", [], [hv(dst, h)], [], 0.0, sem="ar%d%d" % (vis, h), lat=COST["LINK"], after=s, last=last)
        if PAR["m1"] == "V":
            m1 = hv("m1", h)
            tt(m1, ind(v("X%d" % h, 0, W + H), cw), near(h, X1), addo)
        else:
            m1 = v(bank(h), 0, H)
            gather(hv("m1", h), ind(v("X%d" % h, 0, W + H), cw))
            mm([(m1, [(Ib, near(h, X1)), (Ib, hv("m1", h))])])
        if not last:
            affine(hv("m2", h), m1, 0.5, -0.25)
            if PAR["t4"]:
                act(hv("sg", h, 8), hv("cwi", h, 8), ACT.Sign, scale=-1.0, bias=W - 0.5)
            else:
                ts(hv("sg", h, 8), hv("cwi", h, 8), float(W), ALU.is_lt)
        else:
            affine(hv("m16", h), m1, 0.5, 1023.75)
            b = bank(h); Y = hv("Y", h, W)
            mm([(v(b, 0, H), [(sel("LBb", 1), hv("m16", h)), (sel("LBf", 0), hv("Of", h))])])
            act(hv("ys", h), v(b, 0, H), ACT.Identity, bias=yb)
            cp(ind(Y, hv("cl", h, 144, H, H + 8)), hv("ys", h))
            for j, (name, out) in enumerate((("oq", T.yq), ("ox", T.yx))):
                dma("YS"[j * h], "%s%d" % (name, h), lambda a, j=j, out=out: (out[4 * h:4 * h + 4, K * a:K * a + K],
                    T.Y[64 * a + j:64 * a + 64:16, W * h + K * a:W * h + K * a + K]), [], [Y], 2000)
            dma("YS"[h * PAR["os"]], "or%d" % h, lambda a: (T.yr[rows(h), H * a:H * a + H], T.Rf[rows(a), H * h:H * h + H]), [], [hv("Rf", h)], 2000)

    for vis in range(TV):
        for h in range(2):
            jumps(vis, h)
            if vis == TV - 1:
                sums(h)
            rivals(vis, h); scores(vis, h); splice(vis, h)
            if vis < TV - 1:
                stores(vis, h)
        if vis < TV - 1:
            b = bank(1)
            mm([(v(b, 0, 16), [(v("ones"), v("sg"))])])
            if PAR["t4"]:
                act(v("aj"), v(b, 0, 16), ACT.Identity, bias=64 - 0.484375 / 16, scale=0.5, acc=v("Acol", vis + 1, vis + 2))
            else:
                act(v("aj"), v(b, 0, 16), ACT.Identity, bias=-0.484375 / 16, acc=v("Acol", vis + 1, vis + 2))
    return ops


def depend(ops):
    seen = {}
    for i, o in enumerate(ops):
        dep = set()
        for acc, wr in ((o["r"], False), (o["w"], True)):
            for (name, lo, hi, st, a, *_) in acc:
                ps = SCRATCH[name][0] == "psum"
                for (j, l2, h2, s2, w2, a2) in seen.get(name, []):
                    meet = l2 < hi and lo < h2 and (wr or w2) and (a is None or a2 is None or a == a2) and (st != s2 or (lo - l2) % st == 0)
                    if j != i and (meet or (ps and ops[j]["eng"] != o["eng"]) or (ps and ("opt" in o or "opt" in ops[j]))):
                        dep.add(j)
        for acc, wr in ((o["r"], False), (o["w"], True)):
            for (name, lo, hi, st, a, *_) in acc:
                seen.setdefault(name, []).append((i, lo, hi, st, wr, a))
        o["sdep"] = dep | ({o["after"]["id"]} if "after" in o else set())
        if o.get("late"):
            o["sdep"] |= {j for j in range(i) if ops[j].get("remote") and ops[j]["vis"] < o["vis"]}
        o["dep"] = {j for j in dep if ops[j]["eng"] != "P"} if o.get("goes_on") else dep
        o["id"] = i
    anc = []
    for o in ops:
        a = 0
        for j in o["sdep"]:
            a |= anc[j]
        o["sdep"] = {j for j in o["sdep"] if not (a >> j) & 1 or ops[j].get("lat")}
        for j in o["sdep"]:
            a |= 1 << j
        anc.append(a)


def chains(ops, succ):
    prio = [0.0] * len(ops)
    for o in reversed(ops):
        prio[o["id"]] = o["cost"] + o.get("lat", 0) + max([prio[j] + COST["HOP"] for j in succ[o["id"]]], default=0.0)
    return prio


def walk(ops, key, succ):
    left = [len(o["sdep"]) for o in ops]; st = [0.0] * len(ops); done = [0.0] * len(ops); eng = [None] * len(ops)
    free = {e: 0.0 for e in "VSPGYN"}; pool = {e: {} for e in free}
    opts = [o.get("opt", {o["eng"]: (None, o["cost"])}) for o in ops]

    def offer(i):
        for e in opts[i]:
            pool[e][i] = max([done[j] + ops[j].get("lat", 0) + (COST["SAME"] if eng[j] == e else COST["HOP"]) for j in ops[i]["sdep"]], default=0.0)

    for i in range(len(ops)):
        if not left[i]:
            offer(i)
    for _ in ops:
        best = None
        for e, p in pool.items():
            for i, r in p.items():
                t = max(r, free[e])
                if e == "V" and len(opts[i]) > 1 and free["S"] < t + PAR["vpen"]:
                    t = max(t, free["S"]) + 1.0
                if best is None or t < best[0]:
                    best = (t, e)
        t, e = best; p = pool[e]
        can = [i for i in p if not (e == "V" and len(opts[i]) > 1 and free["S"] < t + PAR["vpen"] and len(p) > 1)] or list(p)
        i = min((i for i in can if p[i] <= t + PAR["look"]), key=lambda i: (key[i], i), default=min(can, key=lambda i: p[i]))
        if p[i] > t:
            i = min((j for j in can if p[j] <= t and t + opts[j][e][1] <= p[i] + PAR["fill"]), key=lambda j: (key[j], j), default=i)
        st[i] = max(p[i], free[e]); done[i] = free[e] = st[i] + opts[i][e][1]; eng[i] = e
        for q in opts[i]:
            del pool[q][i]
        for j in succ[i]:
            left[j] -= 1
            if not left[j]:
                offer(j)
    return st, done, eng


def place(ops, key, pred, succ, back):
    left = [len(p) for p in pred]; st = [0.0] * len(ops); done = [0.0] * len(ops); eng = [None] * len(ops)
    busy = {e: [] for e in "VSPGYN"}
    pool = [i for i in range(len(ops)) if not left[i]]
    while pool:
        i = min(pool, key=lambda j: (key[j], j)); pool.remove(i)
        o = ops[i]; best = None
        for e, (_, cost) in o.get("opt", {o["eng"]: (None, o["cost"])}).items():
            t = o.get("lat", 0) if back else 0.0
            for j in pred[i]:
                t = max(t, done[j] + (COST["SAME"] if eng[j] == e else COST["HOP"]) + (o if back else ops[j]).get("lat", 0))
            gaps = busy[e]; k = len(gaps)
            while k and gaps[k - 1][1] > t:
                k -= 1
            while k < len(gaps) and t + cost > gaps[k][0]:
                t = max(t, gaps[k][1]); k += 1
            mark = t + cost + (PAR["vpen"] if e == "V" else 0.0)
            if best is None or mark < best[0]:
                best = (mark, e, k, t, cost)
        _, e, k, t, cost = best
        busy[e].insert(k, (t, t + cost)); st[i] = t; done[i] = t + cost; eng[i] = e
        for j in succ[i]:
            left[j] -= 1
            if not left[j]:
                pool.append(j)
    return st, done, eng


def refine(ops):
    pred = [sorted(o["sdep"]) for o in ops]; succ = [[] for _ in ops]
    for o in ops:
        for j in pred[o["id"]]:
            succ[j].append(o["id"])
    key = PAR["key"] or [-p - 100.0 * PAR["lead"].get("%s%d%d" % (o["ph"], o["vis"], o["half"]), 0) for p, o in zip(chains(ops, succ), ops)]
    key = [o["id"] - 1e9 if "sem" in o and not o["sdep"] else k for k, o in zip(key, ops)]
    best = None
    for n in range(PAR["rounds"]):
        st, done, eng = walk(ops, key, succ) if PAR["walk"] else place(ops, key, pred, succ, False)
        end = max(d + o.get("lat", 0) for d, o in zip(done, ops))
        if best is None or end < best[0]:
            best = (end, st, eng)
        if n + 1 < PAR["rounds"]:
            key = [-d for d in place(ops, [-d for d in done], succ, pred, True)[1]]
    for o, t, e in zip(ops, best[1], best[2]):
        o["t0"] = t
        if "opt" in o:
            o["eng"] = e; o["fns"], o["cost"] = o["opt"][e]
    return sorted(range(len(ops)), key=lambda i: (best[1][i], i)), best[0]


def guesses(T):
    out = []; base = dict(COST)
    for m in GUESS:
        COST.update(m); ops = build(T, None); m = dict(COST); COST.update(base)
        cost = [{e: c[1] for e, c in o["opt"].items()} if "opt" in o else {o["eng"]: o["cost"]} for o in ops]
        out.append((m, cost, [o.get("lat", 0) for o in ops], [o.get("bytes", 0) for o in ops]))
    return out


def play(seq, eng, pred, guess, was, start):
    m, cost, lat, size = guess
    same, hop, wake, d0, d1, rate = m["SAME"], m["HOP"], m["WAKE"], m["D0"], m["D1"], m["RATE"]
    end, fin = list(was[0]), list(was[1]); free = dict.fromkeys("VSPGYN", 0.0); ring = 0.0
    for i in seq[:start]:
        free[eng[i]] = end[i]
        if size[i]:
            ring = fin[i] - d1
    for i in seq[start:]:
        e = eng[i]; t = free[e]; w = wake if e == "G" else 0.0
        for j in pred[i]:
            x = fin[j] + (same if eng[j] == e else hop) + w
            if x > t:
                t = x
        t += cost[i][e]; free[e] = end[i] = t
        if size[i]:
            ring = max(ring, t + d0) + size[i] / rate; fin[i] = ring + d1
        else:
            fin[i] = t + lat[i]
    return end, fin


def anneal(ops, seq, T):
    n = len(ops); pred = [sorted(o["sdep"]) for o in ops]; succ = [[] for _ in ops]
    for o in ops:
        for j in pred[o["id"]]:
            succ[j].append(o["id"])
    eng = [o["eng"] for o in ops]; either = [i for i, o in enumerate(ops) if "opt" in o]; gs = guesses(T); x = [PAR["seed"]]

    def rnd():
        x[0] = (x[0] * 6364136223846793005 + 1442695040888963407) % (1 << 64)
        return ((x[0] >> 11) + 1) / float((1 << 53) + 1)

    now = [play(seq, eng, pred, g, ([0.0] * n, [0.0] * n), 0) for g in gs]
    unit = [max(a[1]) for a in now]; cur = 1.0; best = (cur, seq, eng); steps = PAR["steps"]
    for it in range(steps):
        s, e = seq, eng
        if it % 100 == 0:
            k = it // 100 % len(gs); end, fin = now[k]; before = {}; last = {}
            for i in seq:
                before[i] = last.get(eng[i]); last[eng[i]] = i
            i = fin.index(max(fin)); hot = []
            while i is not None:
                hot.append(i); b = before[i]
                i = max(pred[i], key=lambda j: fin[j], default=None)
                if b is not None and (i is None or end[b] > fin[i] + gs[k][0]["SAME"]):
                    i = b
            hot2 = [i for i in hot if "opt" in ops[i]] or either
        aim = rnd() < PAR["aim"]
        if rnd() < 0.15:
            i = (hot2 if aim else either)[int(rnd() * len(hot2 if aim else either))]; q = p = seq.index(i); e = list(eng); e[i] = "V" if e[i] == "S" else "S"
            near = [k for k in range(max(0, p - 25), min(n, p + 25)) if "opt" in ops[seq[k]] and eng[seq[k]] == e[i]]
            if near and rnd() < 0.6:
                q = near[int(rnd() * len(near))]; e[seq[q]] = eng[i]
        else:
            p = seq.index(hot[int(rnd() * len(hot))]) if aim else int(rnd() * n); i = seq[p]; lo, hi = max(0, p - 40), min(n, p + 41); pos = {seq[k]: k for k in range(lo, hi)}
            far = int(-math.log(rnd()) / 0.7)
            if rnd() < 0.5:
                c = [k for k in range(max([pos[j] + 1 for j in pred[i] if j in pos] + [lo]), p) if eng[seq[k]] == eng[i]][::-1]
            else:
                c = [k for k in range(p + 1, min([pos[j] for j in succ[i] if j in pos] + [hi])) if eng[seq[k]] == eng[i]]
            if not c or ops[i].get("load"):
                continue
            q = c[min(far, len(c) - 1)]
            if ops[seq[q]].get("load"):
                continue
            s = seq[:q] + [i] + seq[q:p] + seq[p + 1:] if q < p else seq[:p] + seq[p + 1:q + 1] + [i] + seq[q + 1:]
        room = -len(gs) * PAR["heat"] * 0.1 ** (it / steps) * math.log(rnd()); new = []; loss = 0.0
        for g, a, u in zip(gs, now, unit):
            new.append(play(s, e, pred, g, a, min(p, q))); loss += (max(new[-1][1]) - max(a[1])) / u
            if loss > room + 0.002:
                break
        if loss <= room:
            cur, seq, eng, now = cur + loss / len(gs), s, e, new
            if cur < best[0]:
                best = (cur, s, e)
    return best[1], best[2]


ORDER = []


def arrange(T, send):
    ops = build(T, send)
    depend(ops)
    if not ORDER:
        ORDER.extend(anneal(ops, refine(ops)[0], T))
    seq, eng = ORDER
    for k, i in enumerate(seq):
        o = ops[i]; o["t0"] = k
        if "opt" in o:
            o["eng"] = eng[i]; o["fns"] = o["opt"][eng[i]][0]
    return ops, seq


def rank_program(g, core, T, topo):
    rank = T.rank_of(core)
    if rank is None:
        return
    cores = list(T.cores); n = len(cores)

    def lanes(src, dst):
        return topo.engines(src, dst)[:8]

    def peer(last, sign):
        return cores[(rank + sign * (-(TV - 1) if last else 1)) % n]

    sent = [0]

    def send(q, out_ap, in_ap, sem, last):
        d = peer(last, 1); rid, pid = topo.addr(d, core); es = lanes(core, d)
        q.remote_dma(out_ap, in_ap, T.sem[sem], T.sem["sent"], pid, rid, sum(1 << e for e in es))
        sent[0] += len(es)

    ops, seq = arrange(T, send)
    queue = {"V": g.vector, "S": g.scalar, "P": g.tensor, "G": g, "Y": g.sync}
    count = {e: 0 for e in "VSPG"}; known = {e: {} for e in "VSPGY"}; total = {}; alone = [False]
    for i in seq:
        o = ops[i]; e = o["eng"]
        if e == "N":
            o["tok"] = (o["sem"], len(lanes(peer(o["last"], -1), core))); o["know"] = {}
            total[o["sem"]] = o["tok"][1]
            continue
        q, kn = queue[e], known[e]
        for d in sorted((ops[j] for j in o["dep"] if "tok" in ops[j]), key=lambda d: -d["t0"]):
            s, c = d["tok"]
            if kn.get(s, 0) < c:
                q.wait_ge(T.sem[s], c); kn[s] = c
                for s2, c2 in d["know"].items():
                    kn[s2] = max(kn.get(s2, 0), c2)
        if e == "G" and not o.get("remote"):
            part = o["w"][0][4] is not None
            if (part or alone[0]) and kn.get("cG", 0) < count["G"]:
                q.wait_ge(T.sem["cG"], count["G"]); kn["cG"] = count["G"]
            alone[0] = part
        o["know"] = dict(kn)
        if o.get("remote"):
            o["fns"][0](q)
        elif "sem" in o:
            for f in o["fns"]:
                f(q).then_inc(T.sem[o["sem"]], 16)
            o["tok"] = (o["sem"], 16 * len(o["fns"])); total[o["sem"]] = o["tok"][1]
        else:
            for f in o["fns"][:-1]:
                f(q)
            o["fns"][-1](q).then_inc(T.sem["c" + e], 1); count[e] += 1
            o["tok"] = ("c" + e, count[e]); total["c" + e] = count[e]
    total["sent"] = sent[0]
    for s, c in total.items():
        g.wait_ge(T.sem[s], c)
